import numpy as np
import ml_dtypes


def mxq(x, axis, fmt="e4m3"):
    dtype, down = {"e4m3": (ml_dtypes.float8_e4m3fn, 7), "e5m2": (ml_dtypes.float8_e5m2, 14)}[fmt]
    v = np.moveaxis(np.asarray(x, np.float32).astype(ml_dtypes.bfloat16).astype(np.float64), axis, -1)
    blocks = v.reshape(v.shape[:-1] + (-1, 32))
    amax = np.abs(blocks).max(-1, keepdims=True)
    byte = np.maximum(np.where(amax > 0, np.frexp(amax)[1] - 1 + 127, 0) - down, 1)
    scale = np.exp2(byte - 127.0)
    codes = (blocks / scale).astype(np.float32).astype(dtype).astype(np.float64)
    return np.moveaxis((codes * scale).reshape(v.shape), -1, axis)


WIDE = False


def mx_kscale(k):
    if not WIDE:
        return np.ones(k)
    levels = np.array([10, -10, 5, -5, 0])
    if k % 512:
        return np.exp2(np.random.permutation(np.resize(levels, k // 32))).repeat(32)
    a = np.empty((k // 512, 16))
    for p in range(k // 512):
        a[p, :8] = np.random.permutation(np.resize(levels, 8))
        for g in range(8):
            far = levels[np.abs(levels - a[p, g]) >= 10]
            a[p, g + 8] = far[np.random.randint(len(far))]
    return np.exp2(a.ravel()).repeat(32)


def f64(x):
    return np.asarray(x).astype(np.float64)


def striped(idx):
    return np.tile(idx.reshape(-1, 16).T, (8, 1)).astype(np.uint16)


def unstriped(offs):
    return offs[:16].T.reshape(-1).astype(np.int64)


def striped8(idx):
    return np.concatenate([x.reshape(-1, 16).T for x in idx]).astype(np.uint16)


def runs(offs, k):
    lists = np.stack([offs[16 * r : 16 * r + 16].T.reshape(-1) for r in range(8)]).astype(np.int64)
    return lists[np.arange(k) % 512 // 64]


def pack_weight(w):
    k, n = w.shape
    w = f64(np.asarray(w, np.float32).astype(ml_dtypes.bfloat16)).reshape(k // 32, 32, n)
    amax = np.abs(w).max(1)
    byte = np.clip(np.where(amax > 0, np.frexp(amax)[1] - 1 + 127 - 7, 1), 1, 254)
    scaled = (w * np.exp2(127.0 - byte)[:, None, :]).reshape(k, n).astype(np.float32)
    words = np.ascontiguousarray(scaled.reshape(k // 512, 128, 4, n).transpose(0, 1, 3, 2)).astype(ml_dtypes.float8_e4m3fn).view(np.uint8)
    return words, np.ascontiguousarray(byte.astype(np.uint8).reshape(k // 512, 16, n))


def unpack_weight(words, scales):
    g, p, n, _ = words.shape
    vals = np.ascontiguousarray(words).view(ml_dtypes.float8_e4m3fn).astype(np.float64) * np.repeat(np.exp2(scales.astype(np.float64) - 127.0), 8, axis=1)[..., None]
    return vals.transpose(0, 1, 3, 2).reshape(g * 512, n)


E2M1 = np.array([0.0, 0.5, 1.0, 1.5, 2.0, 3.0, 4.0, 6.0, -0.0, -0.5, -1.0, -1.5, -2.0, -3.0, -4.0, -6.0])


def pack_fp4(w):
    k, n = w.shape
    w = f64(np.asarray(w, np.float32).astype(ml_dtypes.bfloat16)).reshape(k // 32, 32, n)
    amax = np.abs(w).max(1)
    mant, ex = np.frexp(amax / 6.0)
    byte = np.clip(np.where(amax > 0, np.where(mant > 0.5, ex, ex - 1) + 127, 1), 1, 254)
    scaled = (w * np.exp2(127.0 - byte)[:, None, :]).reshape(k, n).astype(np.float32)
    c = np.ascontiguousarray(scaled.reshape(k // 512, 128, 4, n).transpose(0, 1, 3, 2)).astype(ml_dtypes.float4_e2m1fn).view(np.uint8) & 0xF
    words = (c[..., 0::2] | (c[..., 1::2] << 4)).reshape(k // 512, 128, 2 * n)
    return np.ascontiguousarray(words), np.ascontiguousarray(byte.astype(np.uint8).reshape(k // 512, 16, n))


def unpack_fp4(words, scales):
    g, _, n = scales.shape
    words = np.ascontiguousarray(words).reshape(g, 128, n, 2)
    nib = np.empty((g, 128, n, 4), np.uint8)
    nib[..., 0::2] = words & 0xF
    nib[..., 1::2] = words >> 4
    vals = E2M1[nib] * np.repeat(np.exp2(scales.astype(np.float64) - 127.0), 8, axis=1)[..., None]
    return vals.transpose(0, 1, 3, 2).reshape(g * 512, n)


def relu(v):
    return np.maximum(v, 0.0)

def planes(y):
    n, m = y.shape
    v = y.astype(np.float32).astype(ml_dtypes.bfloat16).astype(np.float64).reshape(n // 32, 32, m)
    top = np.abs(v).max(1)
    byte = np.clip(np.where(top > 0, np.frexp(top)[1] - 1 + 127 - 7, 1), 1, 254)
    codes = (v * np.exp2(127.0 - byte)[:, None, :]).reshape(n, m).astype(np.float32).astype(ml_dtypes.float8_e4m3fn).view(np.uint8)
    words = codes.reshape(n // 512, 128, 4, m).transpose(0, 1, 3, 2)
    return np.ascontiguousarray(words), np.ascontiguousarray(byte.astype(np.uint8).reshape(n // 512, 16, m))


K, T, S, N, H, U = 512, 2048, 512, 512, 512, 1024


def setup_inputs():
    n = np.random.standard_normal
    s = mx_kscale(K)[:, None]
    u = mx_kscale(H)
    packed_xT = pack_weight(n((K, T)) * s)
    packed_w2 = pack_fp4(n((K, N)) / np.sqrt(2 * K) / s)
    packed_w3 = pack_fp4(n((H, N)) / np.sqrt(2 * H) / u[:, None])
    return {
        "x_words": packed_xT[0],
        "x_scales": packed_xT[1],
        "w1": (n((K, H)) / np.sqrt(K) / s * u).astype(np.float32),
        "gain": np.random.uniform(0.3, 1.5, (H, U)).astype(np.float32),
        "w2_words": packed_w2[0],
        "w2_scales": packed_w2[1],
        "w3_words": packed_w3[0],
        "w3_scales": packed_w3[1],
        "offs": striped(np.random.permutation(T)[:S]),
        "ad": striped8(np.stack([np.random.permutation(U)[(U * np.random.uniform(0, 1, S) ** 4).astype(np.int64)] for _ in range(8)])),
    }


def reference(x_words, x_scales, w1, gain, w2_words, w2_scales, w3_words, w3_scales, offs, ad):
    xq = unpack_weight(x_words, x_scales)[:, unstriped(offs)]
    h = relu(mxq(f64(w1), 0, "e4m3").T @ xq)
    z = h * (f64(gain)[np.arange(H)[:, None], runs(ad, H)])
    out_0 = unpack_fp4(w2_words, w2_scales).T @ xq + unpack_fp4(w3_words, w3_scales).T @ mxq(z, 0, "e4m3")
    return (out_0,) + planes(out_0)

@@ -1,0 +1,217 @@
+from contextlib import ExitStack
+
+import concourse.mybir as mybir
+
+K, T, S, N, H, U = 512, 2048, 512, 512, 512, 1024
+FLOPS = 3 * 2 * 512 * 512 * 512
+
+F32 = mybir.dt.float32
+BF16 = mybir.dt.bfloat16
+I32 = mybir.dt.int32
+U32 = mybir.dt.uint32
+U16 = mybir.dt.uint16
+U8 = mybir.dt.uint8
+FP8X4 = mybir.dt.float8_e4m3fn_x4
+FP4X4 = mybir.dt.float4_e2m1fn_x4
+MULT = mybir.AluOpType.mult
+RELU = mybir.ActivationFunctionType.Relu
+
+P = 128
+PACK = 4
+CHUNK = 128
+CHUNKS = S // CHUNK
+HALF = S // 2
+
+
+def tile_picked_slorah_relu_po_kernel(
+    tc, x_words, x_scales, w1, gain, w2_words, w2_scales, w3_words, w3_scales, offs, ad, out_0, out_1, out_2
+):
+    nc = tc.nc
+    with ExitStack() as ctx:
+        keep = ctx.enter_context(tc.tile_pool(name="keep", bufs=1))
+        ring = ctx.enter_context(tc.tile_pool(name="ring", bufs=2))
+
+        offs_sb = keep.tile([P, S // 16], U16, name="offs_sb")
+        ad_sb = keep.tile([P, S // 16], U16, name="ad_sb")
+        x_table = keep.tile([P, T], I32, name="x_table")
+        xs_table = keep.tile([P, T], U8, name="xs_table")
+        w_raw = keep.tile([P, 2, 2 * N], U8, name="w_raw")
+        ws_raw = [keep.tile([P, N], U8, name="ws_raw%d" % w) for w in range(2)]
+        w1_raw = keep.tile([P, PACK, H], F32, name="w1_raw")
+        gains = [keep.tile([P, U], F32, name="gain%d" % t) for t in range(PACK)]
+        warm = keep.tile([P, 2], F32, name="warm")
+
+        nc.vector.memset(xs_table[:].bitcast(I32), 0)
+        nc.vector.memset(warm[:, 0:1], 0.0)
+        for w in range(2):
+            nc.vector.memset(ws_raw[w][:].bitcast(I32), 0)
+
+        def load_scales(queue, tile, rows):
+            for q in range(4):
+                queue.dma_start(tile[32 * q : 32 * q + 4, :].bitcast(I32), rows[0, 4 * q : 4 * q + 4, :].bitcast(I32))
+
+        gain_rows = gain.rearrange("(p t) u -> p t u", t=PACK)
+        nc.sync.dma_start(offs_sb[:], offs)
+        nc.sync.dma_start(w_raw[:, 0, :].bitcast(I32), w2_words[0].bitcast(I32))
+        nc.sync.dma_start(w_raw[:, 1, :].bitcast(I32), w3_words[0].bitcast(I32))
+        nc.sync.dma_start(w1_raw[:], w1.rearrange("(p j) c -> p j c", j=PACK))
+        nc.sync.dma_start(x_table[:], x_words[0].rearrange("p n t -> p (n t)").bitcast(I32))
+        nc.sync.dma_start(ad_sb[:], ad)
+        for t in range(PACK):
+            nc.sync.dma_start(gains[t][:], gain_rows[:, t, :])
+        load_scales(nc.scalar, xs_table, x_scales)
+        nc.scalar.activation(warm[:, 1:2], warm[:, 0:1], RELU)
+        load_scales(nc.scalar, ws_raw[0], w2_scales)
+        load_scales(nc.gpsimd, ws_raw[1], w3_scales)
+
+        w_dealt = keep.tile([P, 2, PACK, 2 * P], U8, name="w_dealt", align_bytes=64)
+        nc.vector.tensor_copy(
+            w_dealt[:].rearrange("p w t (m b) -> p w t m b", b=2),
+            w_raw[:].rearrange("p w (m t b) -> p w t m b", t=PACK, b=2),
+        )
+        xs = keep.tile([P, S], U8, name="xs", align_bytes=64)
+        nc.vector.tensor_copy(xs[:], xs_table[:].indirect(offs_sb[:]))
+
+        w1_pairs = w1_raw[:].rearrange("p j (m u e) -> p u m e j", u=2, e=2)
+        w1_bf = [keep.tile([P, 2, P, PACK], BF16, name="w1_bf%d" % u, align_bytes=64) for u in range(2)]
+        w1_q = keep.tile([P, PACK * P], U32, name="w1_q", align_bytes=64)
+        w1_s = keep.tile([P, PACK * P], U8, name="w1_s", align_bytes=64)
+        nc.vector.tensor_copy(w1_bf[0][:].rearrange("p e m j -> p m e j"), w1_pairs[:, 0])
+        nc.scalar.copy(w1_bf[1][:].rearrange("p e m j -> p m e j"), w1_pairs[:, 1])
+
+        def quantise_w1(u):
+            cols = slice(2 * P * u, 2 * P * (u + 1))
+            nc.vector.quantize_mx(
+                out=w1_q[:, cols].bitcast(FP8X4), scales=w1_s[:, cols], in_=w1_bf[u][:].rearrange("p e m j -> p (e m j)")
+            )
+
+        ws_dealt = keep.tile([P, 2, PACK, P], U8, name="ws_dealt", align_bytes=64)
+        quantise_w1(0)
+        for w in range(2):
+            nc.vector.tensor_copy(ws_dealt[:, w], ws_raw[w][:].rearrange("p (m t) -> p t m", t=PACK))
+        quantise_w1(1)
+
+        xq = keep.tile([P, S], I32, name="xq", align_bytes=64)
+        for half in range(2):
+            nc.vector.tensor_copy(
+                xq[:, half * HALF : (half + 1) * HALF].bitcast(U32),
+                x_table[:].bitcast(U32).indirect(offs_sb[:, half * HALF // 16 : (half + 1) * HALF // 16]),
+            )
+
+        z = keep.tile([P, PACK, S], F32, name="z")
+
+        def hidden(pool, h, t, lo, hi):
+            bank = pool.tile([P, S], F32, name="h_bank")
+            nc.tensor.matmul_mx(
+                out=bank[:, 0 : hi - lo],
+                lhsT=w1_q[:, t * P : (t + 1) * P].bitcast(FP8X4),
+                lhsT_scale=w1_s[:, t * P : (t + 1) * P],
+                rhs=xq[:, lo:hi].bitcast(FP8X4),
+                rhs_scale=xs[:, lo:hi],
+                start=True,
+                stop=True,
+            )
+            nc.scalar.activation(h[:, lo:hi], bank[:, 0 : hi - lo], RELU)
+
+        def gated(h, t, lo, hi):
+            nc.vector.tensor_tensor(
+                z[:, t, lo:hi], gains[t][:].indirect(ad_sb[:, lo // 16 : hi // 16]), h[:, lo:hi], MULT
+            )
+
+        with tc.psum_pool(name="h_psum", bufs=2) as h_psum:
+            for t in range(PACK):
+                h = ring.tile([P, S], F32, name="h")
+                pieces = [(0, HALF), (HALF, S)] if t == 0 else [(0, S)]
+                for lo, hi in pieces:
+                    hidden(h_psum, h, t, lo, hi)
+                if t < PACK - 1:
+                    for lo, hi in pieces:
+                        gated(h, t, lo, hi)
+
+        y_psum = ctx.enter_context(tc.psum_pool(name="y_psum", bufs=1))
+        banks = [[y_psum.tile([P, 2, CHUNK], F32, name="y_bank%d%d" % (c, u)) for u in range(2)] for c in range(CHUNKS)]
+
+        z_bf = [keep.tile([P, CHUNK, PACK], BF16, name="z_bf%d" % c, align_bytes=64) for c in range(CHUNKS)]
+        z_q = [keep.tile([P, CHUNK], U32, name="z_q%d" % c, align_bytes=64) for c in range(CHUNKS)]
+        z_s = [keep.tile([P, CHUNK], U8, name="z_s%d" % c, align_bytes=64) for c in range(CHUNKS)]
+        y = [keep.tile([P, PACK, CHUNK], F32, name="y%d" % c) for c in range(CHUNKS)]
+        y_bf = [keep.tile([P, CHUNK, PACK], BF16, name="y_bf%d" % c, align_bytes=64) for c in range(CHUNKS)]
+        y_q = keep.tile([P, S], I32, name="y_q", align_bytes=64)
+        y_s = keep.tile([P, S], U8, name="y_s", align_bytes=64)
+        out_rows = out_0.rearrange("(p t) j -> p t j", t=PACK)
+        out_words = out_1[0].rearrange("p n t -> p (n t)").bitcast(I32)
+
+        def cols(c):
+            return slice(c * CHUNK, (c + 1) * CHUNK)
+
+        def weave(copy, dst, src):
+            copy(dst.rearrange("p (c i) t -> p c t i", i=4), src.rearrange("p t (c i) -> p c t i", i=4))
+
+        def quantise(codes, scales, src):
+            nc.vector.quantize_mx(out=codes.bitcast(FP8X4), scales=scales, in_=src.rearrange("p n t -> p (n t)"))
+
+        def base_pass(c, t):
+            nc.tensor.matmul_mx(
+                out=banks[c][t // 2][:, t % 2, :],
+                lhsT=w_dealt[:, 0, t, :].bitcast(FP4X4),
+                lhsT_scale=ws_dealt[:, 0, t, :],
+                rhs=xq[:, cols(c)].bitcast(FP8X4),
+                rhs_scale=xs[:, cols(c)],
+                start=True,
+                stop=False,
+            )
+
+        def adapter_pass(c, t):
+            nc.tensor.matmul_mx(
+                out=banks[c][t // 2][:, t % 2, :],
+                lhsT=w_dealt[:, 1, t, :].bitcast(FP4X4),
+                lhsT_scale=ws_dealt[:, 1, t, :],
+                rhs=z_q[c][:].bitcast(FP8X4),
+                rhs_scale=z_s[c][:],
+                start=False,
+                stop=True,
+            )
+
+        def product(c):
+            for u in range(2):
+                adapter_pass(c, 2 * u)
+                base_pass(c, 2 * u + 1)
+                adapter_pass(c, 2 * u + 1)
+                nc.scalar.copy(y[c][:, 2 * u : 2 * u + 2, :], banks[c][u][:])
+            nc.sync.dma_start(out_rows[:, :, cols(c)], y[c][:])
+
+        for c in range(CHUNKS):
+            for u in range(2):
+                base_pass(c, 2 * u)
+
+        def weave_z(c, copy):
+            weave(copy, z_bf[c][:], z[:, :, cols(c)])
+
+        def quantise_z(c):
+            quantise(z_q[c][:], z_s[c][:], z_bf[c][:])
+
+        gated(h, 3, 0, CHUNK)
+        weave_z(0, nc.scalar.copy)
+        gated(h, 3, CHUNK, 2 * CHUNK)
+        weave_z(1, nc.scalar.copy)
+        gated(h, 3, 2 * CHUNK, 3 * CHUNK)
+        quantise_z(0)
+        product(0)
+        gated(h, 3, 3 * CHUNK, 4 * CHUNK)
+        weave_z(2, nc.vector.tensor_copy)
+        quantise_z(1)
+        product(1)
+        weave_z(3, nc.vector.tensor_copy)
+        quantise_z(2)
+        product(2)
+        quantise_z(3)
+        product(3)
+        for c in range(CHUNKS):
+            weave(nc.vector.tensor_copy, y_bf[c][:], y[c][:])
+            quantise(y_q[:, cols(c)], y_s[:, cols(c)], y_bf[c][:])
+            if c >= CHUNKS - 2:
+                done = slice(0, S - CHUNK) if c == CHUNKS - 2 else cols(c)
+                nc.sync.dma_start(out_words[:, done], y_q[:, done])
+        for q in range(4):
+            queue = nc.scalar if q % 2 == 0 else nc.sync
+            queue.dma_start(out_2[0, 4 * q : 4 * q + 4, :].bitcast(I32), y_s[32 * q : 32 * q + 4, :].bitcast(I32))

@@ -21,6 +21,7 @@ PACK = 4
 CHUNK = 128
 CHUNKS = S // CHUNK
 HALF = S // 2
+HEAD = [(0, HALF), (HALF, S)]
 
 
 def tile_picked_slorah_relu_po_kernel(
@@ -46,23 +47,24 @@ def tile_picked_slorah_relu_po_kernel(
         for w in range(2):
             nc.vector.memset(ws_raw[w][:].bitcast(I32), 0)
 
-        def load_scales(queue, tile, rows):
-            for q in range(4):
+        def load_scales(queue, tile, rows, quadrants=range(4)):
+            for q in quadrants:
                 queue.dma_start(tile[32 * q : 32 * q + 4, :].bitcast(I32), rows[0, 4 * q : 4 * q + 4, :].bitcast(I32))
 
         gain_rows = gain.rearrange("(p t) u -> p t u", t=PACK)
+        load_scales(nc.scalar, xs_table, x_scales, range(2))
+        nc.scalar.activation(warm[:, 1:2], warm[:, 0:1], RELU)
         nc.sync.dma_start(offs_sb[:], offs)
         nc.sync.dma_start(w_raw[:, 0, :].bitcast(I32), w2_words[0].bitcast(I32))
         nc.sync.dma_start(w_raw[:, 1, :].bitcast(I32), w3_words[0].bitcast(I32))
+        load_scales(nc.sync, xs_table, x_scales, range(2, 4))
         nc.sync.dma_start(w1_raw[:], w1.rearrange("(p j) c -> p j c", j=PACK))
+        load_scales(nc.sync, ws_raw[0], w2_scales)
         nc.sync.dma_start(x_table[:], x_words[0].rearrange("p n t -> p (n t)").bitcast(I32))
         nc.sync.dma_start(ad_sb[:], ad)
+        load_scales(nc.sync, ws_raw[1], w3_scales)
         for t in range(PACK):
             nc.sync.dma_start(gains[t][:], gain_rows[:, t, :])
-        load_scales(nc.scalar, xs_table, x_scales)
-        nc.scalar.activation(warm[:, 1:2], warm[:, 0:1], RELU)
-        load_scales(nc.scalar, ws_raw[0], w2_scales)
-        load_scales(nc.gpsimd, ws_raw[1], w3_scales)
 
         w_dealt = keep.tile([P, 2, PACK, 2 * P], U8, name="w_dealt", align_bytes=64)
         nc.vector.tensor_copy(
@@ -86,17 +88,21 @@ def tile_picked_slorah_relu_po_kernel(
             )
 
         ws_dealt = keep.tile([P, 2, PACK, P], U8, name="ws_dealt", align_bytes=64)
-        quantise_w1(0)
-        for w in range(2):
+
+        def deal_scales(w):
             nc.vector.tensor_copy(ws_dealt[:, w], ws_raw[w][:].rearrange("p (m t) -> p t m", t=PACK))
+
+        quantise_w1(0)
+        deal_scales(0)
         quantise_w1(1)
 
         xq = keep.tile([P, S], I32, name="xq", align_bytes=64)
-        for half in range(2):
+        for lo, hi in HEAD:
             nc.vector.tensor_copy(
-                xq[:, half * HALF : (half + 1) * HALF].bitcast(U32),
-                x_table[:].bitcast(U32).indirect(offs_sb[:, half * HALF // 16 : (half + 1) * HALF // 16]),
+                xq[:, lo:hi].bitcast(U32), x_table[:].bitcast(U32).indirect(offs_sb[:, lo // 16 : hi // 16])
             )
+
+        deal_scales(1)
 
         z = keep.tile([P, PACK, S], F32, name="z")
 
@@ -121,7 +127,7 @@ def tile_picked_slorah_relu_po_kernel(
         with tc.psum_pool(name="h_psum", bufs=2) as h_psum:
             for t in range(PACK):
                 h = ring.tile([P, S], F32, name="h")
-                pieces = [(0, HALF), (HALF, S)] if t == 0 else [(0, S)]
+                pieces = HEAD if t == 0 else [(0, S)]
                 for lo, hi in pieces:
                     hidden(h_psum, h, t, lo, hi)
                 if t < PACK - 1:
@@ -190,22 +196,11 @@ def tile_picked_slorah_relu_po_kernel(
         def quantise_z(c):
             quantise(z_q[c][:], z_s[c][:], z_bf[c][:])
 
-        gated(h, 3, 0, CHUNK)
-        weave_z(0, nc.scalar.copy)
-        gated(h, 3, CHUNK, 2 * CHUNK)
-        weave_z(1, nc.scalar.copy)
-        gated(h, 3, 2 * CHUNK, 3 * CHUNK)
-        quantise_z(0)
-        product(0)
-        gated(h, 3, 3 * CHUNK, 4 * CHUNK)
-        weave_z(2, nc.vector.tensor_copy)
-        quantise_z(1)
-        product(1)
-        weave_z(3, nc.vector.tensor_copy)
-        quantise_z(2)
-        product(2)
-        quantise_z(3)
-        product(3)
+        for c in range(CHUNKS):
+            gated(h, 3, c * CHUNK, (c + 1) * CHUNK)
+            weave_z(c, nc.vector.tensor_copy if c in (0, CHUNKS - 1) else nc.scalar.copy)
+            quantise_z(c)
+            product(c)
         for c in range(CHUNKS):
             weave(nc.vector.tensor_copy, y_bf[c][:], y[c][:])
             quantise(y_q[:, cols(c)], y_s[:, cols(c)], y_bf[c][:])

@@ -30,19 +30,20 @@ def tile_picked_slorah_relu_po_kernel(
     nc = tc.nc
     with ExitStack() as ctx:
         keep = ctx.enter_context(tc.tile_pool(name="keep", bufs=1))
-        ring = ctx.enter_context(tc.tile_pool(name="ring", bufs=2))
+        ring = ctx.enter_context(tc.tile_pool(name="ring", bufs=3))
 
         offs_sb = keep.tile([P, S // 16], U16, name="offs_sb")
         ad_sb = keep.tile([P, S // 16], U16, name="ad_sb")
         x_table = keep.tile([P, T], I32, name="x_table")
         xs_table = keep.tile([P, T], U8, name="xs_table")
-        w_raw = keep.tile([P, 2, 2 * N], U8, name="w_raw")
+        w_raw = [keep.tile([P, 2 * N], U8, name="w_raw%d" % w) for w in range(2)]
         ws_raw = [keep.tile([P, N], U8, name="ws_raw%d" % w) for w in range(2)]
         w1_raw = keep.tile([P, PACK, H], F32, name="w1_raw")
         gains = [keep.tile([P, U], F32, name="gain%d" % t) for t in range(PACK)]
         warm = keep.tile([P, 2], F32, name="warm")
 
-        nc.vector.memset(xs_table[:].bitcast(I32), 0)
+        nc.gpsimd.memset(xs_table[:, 0:1024].bitcast(I32), 0)
+        nc.vector.memset(xs_table[:, 1024:T].bitcast(I32), 0)
         nc.vector.memset(warm[:, 0:1], 0.0)
         for w in range(2):
             nc.vector.memset(ws_raw[w][:].bitcast(I32), 0)
@@ -55,8 +56,8 @@ def tile_picked_slorah_relu_po_kernel(
         load_scales(nc.scalar, xs_table, x_scales, range(2))
         nc.scalar.activation(warm[:, 1:2], warm[:, 0:1], RELU)
         nc.sync.dma_start(offs_sb[:], offs)
-        nc.sync.dma_start(w_raw[:, 0, :].bitcast(I32), w2_words[0].bitcast(I32))
-        nc.sync.dma_start(w_raw[:, 1, :].bitcast(I32), w3_words[0].bitcast(I32))
+        nc.sync.dma_start(w_raw[0][:].bitcast(I32), w2_words[0].bitcast(I32))
+        nc.sync.dma_start(w_raw[1][:].bitcast(I32), w3_words[0].bitcast(I32))
         load_scales(nc.sync, xs_table, x_scales, range(2, 4))
         nc.sync.dma_start(w1_raw[:], w1.rearrange("(p j) c -> p j c", j=PACK))
         load_scales(nc.sync, ws_raw[0], w2_scales)
@@ -66,11 +67,12 @@ def tile_picked_slorah_relu_po_kernel(
         for t in range(PACK):
             nc.sync.dma_start(gains[t][:], gain_rows[:, t, :])
 
-        w_dealt = keep.tile([P, 2, PACK, 2 * P], U8, name="w_dealt", align_bytes=64)
-        nc.vector.tensor_copy(
-            w_dealt[:].rearrange("p w t (m b) -> p w t m b", b=2),
-            w_raw[:].rearrange("p w (m t b) -> p w t m b", t=PACK, b=2),
-        )
+        w_dealt = [keep.tile([P, PACK, 2 * P], U8, name="w_dealt%d" % w, align_bytes=64) for w in range(2)]
+        for w, engine in enumerate((nc.vector, nc.vector)):
+            engine.tensor_copy(
+                w_dealt[w][:].rearrange("p t (m b) -> p t m b", b=2),
+                w_raw[w][:].rearrange("p (m t b) -> p t m b", t=PACK, b=2),
+            )
         xs = keep.tile([P, S], U8, name="xs", align_bytes=64)
         nc.vector.tensor_copy(xs[:], xs_table[:].indirect(offs_sb[:]))
 
@@ -135,9 +137,8 @@ def tile_picked_slorah_relu_po_kernel(
                         gated(h, t, lo, hi)
 
         y_psum = ctx.enter_context(tc.psum_pool(name="y_psum", bufs=1))
-        banks = [[y_psum.tile([P, 2, CHUNK], F32, name="y_bank%d%d" % (c, u)) for u in range(2)] for c in range(CHUNKS)]
+        banks = [[y_psum.tile([P, PACK, CHUNK], F32, name="y_bank%d%d" % (c, u)) for u in range(2)] for c in range(CHUNKS)]
 
-        z_bf = [keep.tile([P, CHUNK, PACK], BF16, name="z_bf%d" % c, align_bytes=64) for c in range(CHUNKS)]
         z_q = [keep.tile([P, CHUNK], U32, name="z_q%d" % c, align_bytes=64) for c in range(CHUNKS)]
         z_s = [keep.tile([P, CHUNK], U8, name="z_s%d" % c, align_bytes=64) for c in range(CHUNKS)]
         y = [keep.tile([P, PACK, CHUNK], F32, name="y%d" % c) for c in range(CHUNKS)]
@@ -159,7 +160,7 @@ def tile_picked_slorah_relu_po_kernel(
         def base_pass(c, t):
             nc.tensor.matmul_mx(
                 out=banks[c][t // 2][:, t % 2, :],
-                lhsT=w_dealt[:, 0, t, :].bitcast(FP4X4),
+                lhsT=w_dealt[0][:, t, :].bitcast(FP4X4),
                 lhsT_scale=ws_dealt[:, 0, t, :],
                 rhs=xq[:, cols(c)].bitcast(FP8X4),
                 rhs_scale=xs[:, cols(c)],
@@ -170,7 +171,7 @@ def tile_picked_slorah_relu_po_kernel(
         def adapter_pass(c, t):
             nc.tensor.matmul_mx(
                 out=banks[c][t // 2][:, t % 2, :],
-                lhsT=w_dealt[:, 1, t, :].bitcast(FP4X4),
+                lhsT=w_dealt[1][:, t, :].bitcast(FP4X4),
                 lhsT_scale=ws_dealt[:, 1, t, :],
                 rhs=z_q[c][:].bitcast(FP8X4),
                 rhs_scale=z_s[c][:],
@@ -183,23 +184,30 @@ def tile_picked_slorah_relu_po_kernel(
                 adapter_pass(c, 2 * u)
                 base_pass(c, 2 * u + 1)
                 adapter_pass(c, 2 * u + 1)
-                nc.scalar.copy(y[c][:, 2 * u : 2 * u + 2, :], banks[c][u][:])
+                copy = nc.vector.tensor_copy if c < 2 and u == 1 else nc.scalar.copy
+                copy(y[c][:, 2 * u : 2 * u + 2, :], banks[c][u][:, 0:2, :])
             nc.sync.dma_start(out_rows[:, :, cols(c)], y[c][:])
 
+        for i in range(3):
+            nc.tensor.matmul_mx(
+                out=banks[0][0][:].rearrange("p t n -> p (t n)"),
+                lhsT=w1_q[:, 0:P].bitcast(FP8X4),
+                lhsT_scale=w1_s[:, 0:P],
+                rhs=xq[:].bitcast(FP8X4),
+                rhs_scale=xs[:],
+                start=True,
+                stop=True,
+            )
         for c in range(CHUNKS):
             for u in range(2):
                 base_pass(c, 2 * u)
 
-        def weave_z(c, copy):
-            weave(copy, z_bf[c][:], z[:, :, cols(c)])
-
-        def quantise_z(c):
-            quantise(z_q[c][:], z_s[c][:], z_bf[c][:])
-
         for c in range(CHUNKS):
-            gated(h, 3, c * CHUNK, (c + 1) * CHUNK)
-            weave_z(c, nc.vector.tensor_copy if c in (0, CHUNKS - 1) else nc.scalar.copy)
-            quantise_z(c)
+            if c < 3:
+                gated(h, 3, c * CHUNK, (c + 1) * CHUNK if c < 2 else S)
+            z_bf = keep.tile([P, CHUNK, PACK], BF16, name="z_bf%d" % (0 if c == 2 else c), align_bytes=64)
+            weave(nc.vector.tensor_copy if c == 2 else nc.scalar.copy, z_bf[:], z[:, :, cols(c)])
+            quantise(z_q[c][:], z_s[c][:], z_bf[:])
             product(c)
         for c in range(CHUNKS):
             weave(nc.vector.tensor_copy, y_bf[c][:], y[c][:])

@@ -42,8 +42,7 @@ def tile_picked_slorah_relu_po_kernel(
         gains = [keep.tile([P, U], F32, name="gain%d" % t) for t in range(PACK)]
         warm = keep.tile([P, 2], F32, name="warm")
 
-        nc.gpsimd.memset(xs_table[:, 0:1024].bitcast(I32), 0)
-        nc.vector.memset(xs_table[:, 1024:T].bitcast(I32), 0)
+        nc.vector.memset(xs_table[:].bitcast(I32), 0)
         nc.vector.memset(warm[:, 0:1], 0.0)
         for w in range(2):
             nc.vector.memset(ws_raw[w][:].bitcast(I32), 0)

@@ -3,7 +3,7 @@ from contextlib import ExitStack
 import concourse.mybir as mybir
 
 K, T, S, N, H, U = 512, 2048, 512, 512, 512, 1024
-FLOPS = 3 * 2 * 512 * 512 * 512
+FLOPS = 2 * S * (K * H + K * N + H * N)
 
 F32 = mybir.dt.float32
 BF16 = mybir.dt.bfloat16
@@ -15,49 +15,55 @@ FP8X4 = mybir.dt.float8_e4m3fn_x4
 FP4X4 = mybir.dt.float4_e2m1fn_x4
 MULT = mybir.AluOpType.mult
 RELU = mybir.ActivationFunctionType.Relu
+COPY = mybir.ActivationFunctionType.Copy
 
 P = 128
 PACK = 4
+QUADRANTS = 4
+LIST_ROWS = 16
+HALF = S // 2
 CHUNK = 128
 CHUNKS = S // CHUNK
-HALF = S // 2
-HEAD = [(0, HALF), (HALF, S)]
+RUN = 4
 
 
 def tile_picked_slorah_relu_po_kernel(
     tc, x_words, x_scales, w1, gain, w2_words, w2_scales, w3_words, w3_scales, offs, ad, out_0, out_1, out_2
 ):
     nc = tc.nc
+
+    def span(i, width):
+        return slice(i * width, (i + 1) * width)
+
+    def scale_partitions(q):
+        return slice(32 * q, 32 * q + 4)
+
     with ExitStack() as ctx:
         keep = ctx.enter_context(tc.tile_pool(name="keep", bufs=1))
-        ring = ctx.enter_context(tc.tile_pool(name="ring", bufs=3))
 
-        offs_sb = keep.tile([P, S // 16], U16, name="offs_sb")
-        ad_sb = keep.tile([P, S // 16], U16, name="ad_sb")
+        offs_sb = keep.tile([P, S // LIST_ROWS], U16, name="offs_sb")
+        ad_sb = keep.tile([P, S // LIST_ROWS], U16, name="ad_sb")
         x_table = keep.tile([P, T], I32, name="x_table")
         xs_table = keep.tile([P, T], U8, name="xs_table")
         w_raw = [keep.tile([P, 2 * N], U8, name="w_raw%d" % w) for w in range(2)]
         ws_raw = [keep.tile([P, N], U8, name="ws_raw%d" % w) for w in range(2)]
         w1_raw = keep.tile([P, PACK, H], F32, name="w1_raw")
         gains = [keep.tile([P, U], F32, name="gain%d" % t) for t in range(PACK)]
-        warm = keep.tile([P, 2], F32, name="warm")
 
         nc.vector.memset(xs_table[:].bitcast(I32), 0)
-        nc.vector.memset(warm[:, 0:1], 0.0)
         for w in range(2):
             nc.vector.memset(ws_raw[w][:].bitcast(I32), 0)
 
-        def load_scales(queue, tile, rows, quadrants=range(4)):
+        def load_scales(queue, tile, rows, quadrants=range(QUADRANTS)):
             for q in quadrants:
-                queue.dma_start(tile[32 * q : 32 * q + 4, :].bitcast(I32), rows[0, 4 * q : 4 * q + 4, :].bitcast(I32))
+                queue.dma_start(tile[scale_partitions(q), :].bitcast(I32), rows[0, span(q, 4), :].bitcast(I32))
 
         gain_rows = gain.rearrange("(p t) u -> p t u", t=PACK)
-        load_scales(nc.scalar, xs_table, x_scales, range(2))
-        nc.scalar.activation(warm[:, 1:2], warm[:, 0:1], RELU)
+        load_scales(nc.scalar, xs_table, x_scales, range(QUADRANTS // 2))
         nc.sync.dma_start(offs_sb[:], offs)
         nc.sync.dma_start(w_raw[0][:].bitcast(I32), w2_words[0].bitcast(I32))
         nc.sync.dma_start(w_raw[1][:].bitcast(I32), w3_words[0].bitcast(I32))
-        load_scales(nc.sync, xs_table, x_scales, range(2, 4))
+        load_scales(nc.sync, xs_table, x_scales, range(QUADRANTS // 2, QUADRANTS))
         nc.sync.dma_start(w1_raw[:], w1.rearrange("(p j) c -> p j c", j=PACK))
         load_scales(nc.sync, ws_raw[0], w2_scales)
         nc.sync.dma_start(x_table[:], x_words[0].rearrange("p n t -> p (n t)").bitcast(I32))
@@ -67,8 +73,8 @@ def tile_picked_slorah_relu_po_kernel(
             nc.sync.dma_start(gains[t][:], gain_rows[:, t, :])
 
         w_dealt = [keep.tile([P, PACK, 2 * P], U8, name="w_dealt%d" % w, align_bytes=64) for w in range(2)]
-        for w, engine in enumerate((nc.vector, nc.vector)):
-            engine.tensor_copy(
+        for w in range(2):
+            nc.vector.tensor_copy(
                 w_dealt[w][:].rearrange("p t (m b) -> p t m b", b=2),
                 w_raw[w][:].rearrange("p (m t b) -> p t m b", t=PACK, b=2),
             )
@@ -80,12 +86,13 @@ def tile_picked_slorah_relu_po_kernel(
         w1_q = keep.tile([P, PACK * P], U32, name="w1_q", align_bytes=64)
         w1_s = keep.tile([P, PACK * P], U8, name="w1_s", align_bytes=64)
         nc.vector.tensor_copy(w1_bf[0][:].rearrange("p e m j -> p m e j"), w1_pairs[:, 0])
-        nc.scalar.copy(w1_bf[1][:].rearrange("p e m j -> p m e j"), w1_pairs[:, 1])
+        nc.scalar.activation(w1_bf[1][:].rearrange("p e m j -> p m e j"), w1_pairs[:, 1], COPY)
 
         def quantise_w1(u):
-            cols = slice(2 * P * u, 2 * P * (u + 1))
             nc.vector.quantize_mx(
-                out=w1_q[:, cols].bitcast(FP8X4), scales=w1_s[:, cols], in_=w1_bf[u][:].rearrange("p e m j -> p (e m j)")
+                out=w1_q[:, span(u, 2 * P)].bitcast(FP8X4),
+                scales=w1_s[:, span(u, 2 * P)],
+                in_=w1_bf[u][:].rearrange("p e m j -> p (e m j)"),
             )
 
         ws_dealt = keep.tile([P, 2, PACK, P], U8, name="ws_dealt", align_bytes=64)
@@ -98,46 +105,45 @@ def tile_picked_slorah_relu_po_kernel(
         quantise_w1(1)
 
         xq = keep.tile([P, S], I32, name="xq", align_bytes=64)
-        for lo, hi in HEAD:
+        for half in range(2):
             nc.vector.tensor_copy(
-                xq[:, lo:hi].bitcast(U32), x_table[:].bitcast(U32).indirect(offs_sb[:, lo // 16 : hi // 16])
+                xq[:, span(half, HALF)].bitcast(U32),
+                x_table[:].bitcast(U32).indirect(offs_sb[:, span(half, HALF // LIST_ROWS)]),
             )
-
         deal_scales(1)
 
-        z = keep.tile([P, PACK, S], F32, name="z")
+        z = [keep.tile([P, PACK * HALF], F32, name="z%d" % half, align_bytes=64) for half in range(2)]
 
-        def hidden(pool, h, t, lo, hi):
-            bank = pool.tile([P, S], F32, name="h_bank")
-            nc.tensor.matmul_mx(
-                out=bank[:, 0 : hi - lo],
-                lhsT=w1_q[:, t * P : (t + 1) * P].bitcast(FP8X4),
-                lhsT_scale=w1_s[:, t * P : (t + 1) * P],
-                rhs=xq[:, lo:hi].bitcast(FP8X4),
-                rhs_scale=xs[:, lo:hi],
-                start=True,
-                stop=True,
-            )
-            nc.scalar.activation(h[:, lo:hi], bank[:, 0 : hi - lo], RELU)
+        def z_piece(t, half):
+            return z[half][:, span(t, HALF)]
 
-        def gated(h, t, lo, hi):
-            nc.vector.tensor_tensor(
-                z[:, t, lo:hi], gains[t][:].indirect(ad_sb[:, lo // 16 : hi // 16]), h[:, lo:hi], MULT
-            )
+        pieces = [(0, 0), (0, 1), (1, 0), (2, 0), (3, 0), (3, 1), (1, 1), (2, 1)]
+        h = {(3, 0): z_piece(1, 1)}
+        with tc.psum_pool(name="h_psum", bufs=3) as h_psum:
+            for t, half in pieces:
+                if (t, half) not in h:
+                    h[t, half] = keep.tile([P, HALF], F32, name="h%d%d" % (t, half))[:]
+                h_bank = h_psum.tile([P, HALF], F32, name="h_bank")
+                nc.tensor.matmul_mx(
+                    out=h_bank[:],
+                    lhsT=w1_q[:, span(t, P)].bitcast(FP8X4),
+                    lhsT_scale=w1_s[:, span(t, P)],
+                    rhs=xq[:, span(half, HALF)].bitcast(FP8X4),
+                    rhs_scale=xs[:, span(half, HALF)],
+                    start=True,
+                    stop=True,
+                )
+                nc.scalar.activation(h[t, half], h_bank[:], RELU)
 
-        with tc.psum_pool(name="h_psum", bufs=2) as h_psum:
-            for t in range(PACK):
-                h = ring.tile([P, S], F32, name="h")
-                pieces = HEAD if t == 0 else [(0, S)]
-                for lo, hi in pieces:
-                    hidden(h_psum, h, t, lo, hi)
-                if t < PACK - 1:
-                    for lo, hi in pieces:
-                        gated(h, t, lo, hi)
+        def gate(t, half):
+            entries = ad_sb[:, span(half, HALF // LIST_ROWS)]
+            nc.vector.tensor_tensor(z_piece(t, half), gains[t][:].indirect(entries), h[t, half], MULT)
+
+        for t, half in pieces[:-1]:
+            gate(t, half)
 
         y_psum = ctx.enter_context(tc.psum_pool(name="y_psum", bufs=1))
-        banks = [[y_psum.tile([P, PACK, CHUNK], F32, name="y_bank%d%d" % (c, u)) for u in range(2)] for c in range(CHUNKS)]
-
+        banks = [[y_psum.tile([P, 2, CHUNK], F32, name="y_bank%d%d" % (c, u)) for u in range(2)] for c in range(CHUNKS)]
         z_q = [keep.tile([P, CHUNK], U32, name="z_q%d" % c, align_bytes=64) for c in range(CHUNKS)]
         z_s = [keep.tile([P, CHUNK], U8, name="z_s%d" % c, align_bytes=64) for c in range(CHUNKS)]
         y = [keep.tile([P, PACK, CHUNK], F32, name="y%d" % c) for c in range(CHUNKS)]
@@ -147,73 +153,61 @@ def tile_picked_slorah_relu_po_kernel(
         out_rows = out_0.rearrange("(p t) j -> p t j", t=PACK)
         out_words = out_1[0].rearrange("p n t -> p (n t)").bitcast(I32)
 
-        def cols(c):
-            return slice(c * CHUNK, (c + 1) * CHUNK)
-
         def weave(copy, dst, src):
-            copy(dst.rearrange("p (c i) t -> p c t i", i=4), src.rearrange("p t (c i) -> p c t i", i=4))
+            copy(dst.rearrange("p (c i) t -> p c t i", i=RUN), src.rearrange("p t (c i) -> p c t i", i=RUN))
 
-        def quantise(codes, scales, src):
-            nc.vector.quantize_mx(out=codes.bitcast(FP8X4), scales=scales, in_=src.rearrange("p n t -> p (n t)"))
+        def quantise(codes, scales, woven):
+            nc.vector.quantize_mx(out=codes.bitcast(FP8X4), scales=scales, in_=woven.rearrange("p n t -> p (n t)"))
+
+        def output_pass(w, c, t, codes, scales):
+            nc.tensor.matmul_mx(
+                out=banks[c][t // 2][:, t % 2, :],
+                lhsT=w_dealt[w][:, t, :].bitcast(FP4X4),
+                lhsT_scale=ws_dealt[:, w, t, :],
+                rhs=codes.bitcast(FP8X4),
+                rhs_scale=scales,
+                start=(w == 0),
+                stop=(w == 1),
+            )
 
         def base_pass(c, t):
-            nc.tensor.matmul_mx(
-                out=banks[c][t // 2][:, t % 2, :],
-                lhsT=w_dealt[0][:, t, :].bitcast(FP4X4),
-                lhsT_scale=ws_dealt[:, 0, t, :],
-                rhs=xq[:, cols(c)].bitcast(FP8X4),
-                rhs_scale=xs[:, cols(c)],
-                start=True,
-                stop=False,
-            )
+            output_pass(0, c, t, xq[:, span(c, CHUNK)], xs[:, span(c, CHUNK)])
 
         def adapter_pass(c, t):
-            nc.tensor.matmul_mx(
-                out=banks[c][t // 2][:, t % 2, :],
-                lhsT=w_dealt[1][:, t, :].bitcast(FP4X4),
-                lhsT_scale=ws_dealt[:, 1, t, :],
-                rhs=z_q[c][:].bitcast(FP8X4),
-                rhs_scale=z_s[c][:],
-                start=False,
-                stop=True,
-            )
+            output_pass(1, c, t, z_q[c][:], z_s[c][:])
 
-        def product(c):
-            for u in range(2):
-                adapter_pass(c, 2 * u)
-                base_pass(c, 2 * u + 1)
-                adapter_pass(c, 2 * u + 1)
-                copy = nc.vector.tensor_copy if c < 2 and u == 1 else nc.scalar.copy
-                copy(y[c][:, 2 * u : 2 * u + 2, :], banks[c][u][:, 0:2, :])
-            nc.sync.dma_start(out_rows[:, :, cols(c)], y[c][:])
-
-        for i in range(3):
-            nc.tensor.matmul_mx(
-                out=banks[0][0][:].rearrange("p t n -> p (t n)"),
-                lhsT=w1_q[:, 0:P].bitcast(FP8X4),
-                lhsT_scale=w1_s[:, 0:P],
-                rhs=xq[:].bitcast(FP8X4),
-                rhs_scale=xs[:],
-                start=True,
-                stop=True,
-            )
         for c in range(CHUNKS):
             for u in range(2):
                 base_pass(c, 2 * u)
 
-        for c in range(CHUNKS):
-            if c < 3:
-                gated(h, 3, c * CHUNK, (c + 1) * CHUNK if c < 2 else S)
-            z_bf = keep.tile([P, CHUNK, PACK], BF16, name="z_bf%d" % (0 if c == 2 else c), align_bytes=64)
-            weave(nc.vector.tensor_copy if c == 2 else nc.scalar.copy, z_bf[:], z[:, :, cols(c)])
-            quantise(z_q[c][:], z_s[c][:], z_bf[:])
-            product(c)
-        for c in range(CHUNKS):
+        def finish_chunk(c, copy, woven):
+            planes = z[c // 2][:].rearrange("p (t n) -> p t n", t=PACK)
+            weave(copy, woven, planes[:, :, span(c % 2, CHUNK)])
+            quantise(z_q[c][:], z_s[c][:], woven)
+            for u in range(2):
+                adapter_pass(c, 2 * u)
+                base_pass(c, 2 * u + 1)
+                adapter_pass(c, 2 * u + 1)
+                nc.scalar.copy(y[c][:, span(u, 2), :], banks[c][u][:])
+            nc.sync.dma_start(out_rows[:, :, span(c, CHUNK)], y[c][:])
+
+        finish_chunk(0, nc.scalar.copy, z_piece(2, 1).bitcast(BF16).rearrange("p (n t) -> p n t", t=PACK))
+        z_bf = keep.tile([P, CHUNK, PACK], BF16, name="z_bf", align_bytes=64)
+        finish_chunk(1, nc.scalar.copy, z_bf[:])
+        gate(*pieces[-1])
+        z_bf = keep.tile([P, HALF, PACK], BF16, name="z_bf", align_bytes=64)
+        for c in range(CHUNKS // 2, CHUNKS):
+            finish_chunk(c, nc.vector.tensor_copy, z_bf[:, span(c % 2, CHUNK), :])
+
+        def quantise_y(c):
             weave(nc.vector.tensor_copy, y_bf[c][:], y[c][:])
-            quantise(y_q[:, cols(c)], y_s[:, cols(c)], y_bf[c][:])
-            if c >= CHUNKS - 2:
-                done = slice(0, S - CHUNK) if c == CHUNKS - 2 else cols(c)
-                nc.sync.dma_start(out_words[:, done], y_q[:, done])
-        for q in range(4):
+            quantise(y_q[:, span(c, CHUNK)], y_s[:, span(c, CHUNK)], y_bf[c][:])
+
+        for c in range(CHUNKS - 1):
+            quantise_y(c)
+        nc.sync.dma_start(out_words[:, 0 : S - CHUNK], y_q[:, 0 : S - CHUNK])
+        quantise_y(CHUNKS - 1)
+        nc.sync.dma_start(out_words[:, S - CHUNK : S], y_q[:, S - CHUNK : S])
+        for q in range(QUADRANTS):
             queue = nc.scalar if q % 2 == 0 else nc.sync
-            queue.dma_start(out_2[0, 4 * q : 4 * q + 4, :].bitcast(I32), y_s[32 * q : 32 * q + 4, :].bitcast(I32))
+            queue.dma_start(out_2[0, span(q, 4), :].bitcast(I32), y_s[scale_partitions(q), :].bitcast(I32))

@@ -51,35 +51,38 @@ def tile_picked_slorah_relu_po_kernel(
         gains = [keep.tile([P, U], F32, name="gain%d" % t) for t in range(PACK)]
 
         nc.vector.memset(xs_table[:].bitcast(I32), 0)
-        for w in range(2):
-            nc.vector.memset(ws_raw[w][:].bitcast(I32), 0)
+        xs = keep.tile([P, S], U8, name="xs", align_bytes=64)
+        for tile in (ws_raw[0], ws_raw[1], xs):
+            nc.vector.memset(tile[:].bitcast(I32), 0)
 
         def load_scales(queue, tile, rows, quadrants=range(QUADRANTS)):
             for q in quadrants:
                 queue.dma_start(tile[scale_partitions(q), :].bitcast(I32), rows[0, span(q, 4), :].bitcast(I32))
 
         gain_rows = gain.rearrange("(p t) u -> p t u", t=PACK)
-        load_scales(nc.scalar, xs_table, x_scales, range(QUADRANTS // 2))
         nc.sync.dma_start(offs_sb[:], offs)
         nc.sync.dma_start(w_raw[0][:].bitcast(I32), w2_words[0].bitcast(I32))
         nc.sync.dma_start(w_raw[1][:].bitcast(I32), w3_words[0].bitcast(I32))
-        load_scales(nc.sync, xs_table, x_scales, range(QUADRANTS // 2, QUADRANTS))
+        nc.sync.dma_start(xs_table[0:P:8, :].bitcast(I32), x_scales[0].bitcast(I32))
         nc.sync.dma_start(w1_raw[:], w1.rearrange("(p j) c -> p j c", j=PACK))
         load_scales(nc.sync, ws_raw[0], w2_scales)
         nc.sync.dma_start(x_table[:], x_words[0].rearrange("p n t -> p (n t)").bitcast(I32))
-        nc.sync.dma_start(ad_sb[:], ad)
-        load_scales(nc.sync, ws_raw[1], w3_scales)
-        for t in range(PACK):
-            nc.sync.dma_start(gains[t][:], gain_rows[:, t, :])
 
         w_dealt = [keep.tile([P, PACK, 2 * P], U8, name="w_dealt%d" % w, align_bytes=64) for w in range(2)]
         for w in range(2):
             nc.vector.tensor_copy(
-                w_dealt[w][:].rearrange("p t (m b) -> p t m b", b=2),
-                w_raw[w][:].rearrange("p (m t b) -> p t m b", t=PACK, b=2),
+                w_dealt[w][:].bitcast(U16),
+                w_raw[w][:].bitcast(U16).rearrange("p (m t) -> p t m", t=PACK),
             )
-        xs = keep.tile([P, S], U8, name="xs", align_bytes=64)
-        nc.vector.tensor_copy(xs[:], xs_table[:].indirect(offs_sb[:]))
+        xs_picked = keep.tile([P, S], U8, name="xs_picked", align_bytes=64)
+        nc.vector.tensor_copy(xs_picked[:], xs_table[:].indirect(offs_sb[:]))
+        for q in range(QUADRANTS):
+            nc.sync.dma_start(xs[scale_partitions(q), :].bitcast(I32), xs_picked[32 * q : 32 * q + 32 : 8, :].bitcast(I32))
+        nc.sync.dma_start(ad_sb[:], ad)
+        for t in range(PACK):
+            if t == 2:
+                load_scales(nc.sync, ws_raw[1], w3_scales)
+            nc.sync.dma_start(gains[t][:], gain_rows[:, t, :])
 
         w1_pairs = w1_raw[:].rearrange("p j (m u e) -> p u m e j", u=2, e=2)
         w1_bf = [keep.tile([P, 2, P, PACK], BF16, name="w1_bf%d" % u, align_bytes=64) for u in range(2)]

@@ -24,7 +24,7 @@ LIST_ROWS = 16
 HALF = S // 2
 CHUNK = 128
 CHUNKS = S // CHUNK
-RUN = 4
+RUN = 2
 
 
 def tile_picked_slorah_relu_po_kernel(
@@ -150,7 +150,7 @@ def tile_picked_slorah_relu_po_kernel(
         z_q = [keep.tile([P, CHUNK], U32, name="z_q%d" % c, align_bytes=64) for c in range(CHUNKS)]
         z_s = [keep.tile([P, CHUNK], U8, name="z_s%d" % c, align_bytes=64) for c in range(CHUNKS)]
         y = [keep.tile([P, PACK, CHUNK], F32, name="y%d" % c) for c in range(CHUNKS)]
-        y_bf = [keep.tile([P, CHUNK, PACK], BF16, name="y_bf%d" % c, align_bytes=64) for c in range(CHUNKS)]
+        y_bf = keep.tile([P, S * PACK], BF16, name="y_bf", align_bytes=64)
         y_q = keep.tile([P, S], I32, name="y_q", align_bytes=64)
         y_s = keep.tile([P, S], U8, name="y_s", align_bytes=64)
         out_rows = out_0.rearrange("(p t) j -> p t j", t=PACK)
@@ -202,14 +202,18 @@ def tile_picked_slorah_relu_po_kernel(
         for c in range(CHUNKS // 2, CHUNKS):
             finish_chunk(c, nc.vector.tensor_copy, z_bf[:, span(c % 2, CHUNK), :])
 
-        def quantise_y(c):
-            weave(nc.vector.tensor_copy, y_bf[c][:], y[c][:])
-            quantise(y_q[:, span(c, CHUNK)], y_s[:, span(c, CHUNK)], y_bf[c][:])
+        y_woven = y_bf[:].rearrange("p (n t) -> p n t", t=PACK)
 
-        for c in range(CHUNKS - 1):
-            quantise_y(c)
+        def quantise_y(first, count):
+            for c in range(first, first + count):
+                weave(nc.vector.tensor_copy, y_woven[:, span(c, CHUNK), :], y[c][:])
+            cols = slice(first * CHUNK, (first + count) * CHUNK)
+            quantise(y_q[:, cols], y_s[:, cols], y_woven[:, cols, :])
+
+        quantise_y(0, 2)
+        quantise_y(2, 1)
         nc.sync.dma_start(out_words[:, 0 : S - CHUNK], y_q[:, 0 : S - CHUNK])
-        quantise_y(CHUNKS - 1)
+        quantise_y(3, 1)
         nc.sync.dma_start(out_words[:, S - CHUNK : S], y_q[:, S - CHUNK : S])
         for q in range(QUADRANTS):
             queue = nc.scalar if q % 2 == 0 else nc.sync

@@ -149,7 +149,8 @@ def tile_picked_slorah_relu_po_kernel(
         banks = [[y_psum.tile([P, 2, CHUNK], F32, name="y_bank%d%d" % (c, u)) for u in range(2)] for c in range(CHUNKS)]
         z_q = [keep.tile([P, CHUNK], U32, name="z_q%d" % c, align_bytes=64) for c in range(CHUNKS)]
         z_s = [keep.tile([P, CHUNK], U8, name="z_s%d" % c, align_bytes=64) for c in range(CHUNKS)]
-        y = [keep.tile([P, PACK, CHUNK], F32, name="y%d" % c) for c in range(CHUNKS)]
+        y_halves = [keep.tile([P, PACK, HALF], F32, name="y%d" % half) for half in range(2)]
+        y = [y_halves[c // 2][:, :, span(c % 2, CHUNK)] for c in range(CHUNKS)]
         y_bf = keep.tile([P, S * PACK], BF16, name="y_bf", align_bytes=64)
         y_q = keep.tile([P, S], I32, name="y_q", align_bytes=64)
         y_s = keep.tile([P, S], U8, name="y_s", align_bytes=64)
@@ -192,7 +193,10 @@ def tile_picked_slorah_relu_po_kernel(
                 base_pass(c, 2 * u + 1)
                 adapter_pass(c, 2 * u + 1)
                 nc.scalar.copy(y[c][:, span(u, 2), :], banks[c][u][:])
-            nc.sync.dma_start(out_rows[:, :, span(c, CHUNK)], y[c][:])
+                if c < 2:
+                    nc.sync.dma_start(out_rows[:, span(u, 2), span(c, CHUNK)], y[c][:, span(u, 2), :])
+                elif c == CHUNKS - 1:
+                    nc.sync.dma_start(out_rows[:, span(u, 2), span(1, HALF)], y_halves[1][:, span(u, 2), :])
 
         finish_chunk(0, nc.scalar.copy, z_piece(2, 1).bitcast(BF16).rearrange("p (n t) -> p n t", t=PACK))
         z_bf = keep.tile([P, CHUNK, PACK], BF16, name="z_bf", align_bytes=64)
@@ -206,7 +210,7 @@ def tile_picked_slorah_relu_po_kernel(
 
         def quantise_y(first, count):
             for c in range(first, first + count):
-                weave(nc.vector.tensor_copy, y_woven[:, span(c, CHUNK), :], y[c][:])
+                weave(nc.vector.tensor_copy, y_woven[:, span(c, CHUNK), :], y[c])
             cols = slice(first * CHUNK, (first + count) * CHUNK)
             quantise(y_q[:, cols], y_s[:, cols], y_woven[:, cols, :])
 

@@ -24,6 +24,7 @@ LIST_ROWS = 16
 HALF = S // 2
 CHUNK = 128
 CHUNKS = S // CHUNK
+X_FIRST = 7 * T // 16
 RUN = 2
 
 
@@ -43,69 +44,71 @@ def tile_picked_slorah_relu_po_kernel(
 
         offs_sb = keep.tile([P, S // LIST_ROWS], U16, name="offs_sb")
         ad_sb = keep.tile([P, S // LIST_ROWS], U16, name="ad_sb")
-        x_table = keep.tile([P, T], I32, name="x_table")
+        x_table = keep.tile([P, T], I32, name="x_table", align_bytes=64)
         xs_table = keep.tile([P, T], U8, name="xs_table")
         w_raw = [keep.tile([P, 2 * N], U8, name="w_raw%d" % w) for w in range(2)]
-        ws_raw = [keep.tile([P, N], U8, name="ws_raw%d" % w) for w in range(2)]
+        ws_raw = keep.tile([P, 2 * N], U8, name="ws_raw")
         w1_raw = keep.tile([P, PACK, H], F32, name="w1_raw")
         gains = [keep.tile([P, U], F32, name="gain%d" % t) for t in range(PACK)]
-
-        nc.vector.memset(xs_table[:].bitcast(I32), 0)
         xs = keep.tile([P, S], U8, name="xs", align_bytes=64)
-        for tile in (ws_raw[0], ws_raw[1], xs):
+        ws = keep.tile([P, 2 * N], U8, name="ws", align_bytes=64)
+
+        for tile in (xs_table, ws_raw, xs, ws):
             nc.vector.memset(tile[:].bitcast(I32), 0)
 
-        def load_scales(queue, tile, rows, quadrants=range(QUADRANTS)):
-            for q in quadrants:
-                queue.dma_start(tile[scale_partitions(q), :].bitcast(I32), rows[0, span(q, 4), :].bitcast(I32))
+        def move_scales(dst, src):
+            for q in range(QUADRANTS):
+                nc.sync.dma_start(dst[scale_partitions(q), :].bitcast(I32), src[32 * q : 32 * q + 32 : 8, :].bitcast(I32))
 
         gain_rows = gain.rearrange("(p t) u -> p t u", t=PACK)
+        x_rows = x_words[0].rearrange("p n t -> p (n t)").bitcast(I32)
         nc.sync.dma_start(offs_sb[:], offs)
-        nc.sync.dma_start(w_raw[0][:].bitcast(I32), w2_words[0].bitcast(I32))
-        nc.sync.dma_start(w_raw[1][:].bitcast(I32), w3_words[0].bitcast(I32))
+        nc.sync.dma_start(x_table[:, 0:X_FIRST], x_rows[:, 0:X_FIRST])
+        nc.sync.dma_start(ad_sb[:], ad)
         nc.sync.dma_start(xs_table[0:P:8, :].bitcast(I32), x_scales[0].bitcast(I32))
+        nc.sync.dma_start(ws_raw[0:P:8, span(0, N)].bitcast(I32), w2_scales[0].bitcast(I32))
+        nc.sync.dma_start(ws_raw[0:P:8, span(1, N)].bitcast(I32), w3_scales[0].bitcast(I32))
         nc.sync.dma_start(w1_raw[:], w1.rearrange("(p j) c -> p j c", j=PACK))
-        load_scales(nc.sync, ws_raw[0], w2_scales)
-        nc.sync.dma_start(x_table[:], x_words[0].rearrange("p n t -> p (n t)").bitcast(I32))
+        nc.sync.dma_start(x_table[:, X_FIRST:T], x_rows[:, X_FIRST:T])
 
         w_dealt = [keep.tile([P, PACK, 2 * P], U8, name="w_dealt%d" % w, align_bytes=64) for w in range(2)]
-        for w in range(2):
+
+        def deal_words(w):
             nc.vector.tensor_copy(
                 w_dealt[w][:].bitcast(U16),
                 w_raw[w][:].bitcast(U16).rearrange("p (m t) -> p t m", t=PACK),
             )
+
         xs_picked = keep.tile([P, S], U8, name="xs_picked", align_bytes=64)
         nc.vector.tensor_copy(xs_picked[:], xs_table[:].indirect(offs_sb[:]))
-        for q in range(QUADRANTS):
-            nc.sync.dma_start(xs[scale_partitions(q), :].bitcast(I32), xs_picked[32 * q : 32 * q + 32 : 8, :].bitcast(I32))
-        nc.sync.dma_start(ad_sb[:], ad)
-        for t in range(PACK):
-            if t == 2:
-                load_scales(nc.sync, ws_raw[1], w3_scales)
-            nc.sync.dma_start(gains[t][:], gain_rows[:, t, :])
+        move_scales(xs, xs_picked)
+        nc.sync.dma_start(w_raw[0][:].bitcast(I32), w2_words[0].bitcast(I32))
+        nc.sync.dma_start(w_raw[1][:].bitcast(I32), w3_words[0].bitcast(I32))
 
         w1_pairs = w1_raw[:].rearrange("p j (m u e) -> p u m e j", u=2, e=2)
         w1_bf = [keep.tile([P, 2, P, PACK], BF16, name="w1_bf%d" % u, align_bytes=64) for u in range(2)]
-        w1_q = keep.tile([P, PACK * P], U32, name="w1_q", align_bytes=64)
+        w1_q = [keep.tile([P, 2 * P], U32, name="w1_q", align_bytes=64)]
         w1_s = keep.tile([P, PACK * P], U8, name="w1_s", align_bytes=64)
         nc.vector.tensor_copy(w1_bf[0][:].rearrange("p e m j -> p m e j"), w1_pairs[:, 0])
         nc.scalar.activation(w1_bf[1][:].rearrange("p e m j -> p m e j"), w1_pairs[:, 1], COPY)
 
         def quantise_w1(u):
             nc.vector.quantize_mx(
-                out=w1_q[:, span(u, 2 * P)].bitcast(FP8X4),
+                out=w1_q[u][:].bitcast(FP8X4),
                 scales=w1_s[:, span(u, 2 * P)],
                 in_=w1_bf[u][:].rearrange("p e m j -> p (e m j)"),
             )
 
-        ws_dealt = keep.tile([P, 2, PACK, P], U8, name="ws_dealt", align_bytes=64)
-
-        def deal_scales(w):
-            nc.vector.tensor_copy(ws_dealt[:, w], ws_raw[w][:].rearrange("p (m t) -> p t m", t=PACK))
-
+        ws_dealt = keep.tile([P, 2 * N], U8, name="ws_dealt")
+        nc.vector.tensor_copy(
+            ws_dealt[:].rearrange("p (w t m) -> p w t m", w=2, t=PACK),
+            ws_raw[:].rearrange("p (w m t) -> p w t m", w=2, t=PACK),
+        )
         quantise_w1(0)
-        deal_scales(0)
-        quantise_w1(1)
+        for t in range(PACK):
+            if t == 2:
+                move_scales(ws, ws_dealt)
+            nc.sync.dma_start(gains[t][:], gain_rows[:, t, :])
 
         xq = keep.tile([P, S], I32, name="xq", align_bytes=64)
         for half in range(2):
@@ -113,12 +116,20 @@ def tile_picked_slorah_relu_po_kernel(
                 xq[:, span(half, HALF)].bitcast(U32),
                 x_table[:].bitcast(U32).indirect(offs_sb[:, span(half, HALF // LIST_ROWS)]),
             )
-        deal_scales(1)
+        w1_q.append(keep.tile([P, 2 * P], U32, name="x_table", align_bytes=64))
+        deal_words(0)
+        quantise_w1(1)
+        deal_words(1)
 
-        z = [keep.tile([P, PACK * HALF], F32, name="z%d" % half, align_bytes=64) for half in range(2)]
+        late_step = CHUNK + PACK * HALF
+        early_start = 2 * late_step + CHUNK
+        z_tile = keep.tile([P, PACK * late_step], F32, name="z", align_bytes=64)
+        early = z_tile[:, early_start : early_start + PACK * HALF].rearrange("p (t n) -> p t n", t=PACK)
+        late = z_tile[:].rearrange("p (t n) -> p t n", t=PACK)[:, :, 0:HALF]
+        z = [early, late]
 
         def z_piece(t, half):
-            return z[half][:, span(t, HALF)]
+            return z[half][:, t, :]
 
         pieces = [(0, 0), (0, 1), (1, 0), (2, 0), (3, 0), (3, 1), (1, 1), (2, 1)]
         h = {(3, 0): z_piece(1, 1)}
@@ -129,7 +140,7 @@ def tile_picked_slorah_relu_po_kernel(
                 h_bank = h_psum.tile([P, HALF], F32, name="h_bank")
                 nc.tensor.matmul_mx(
                     out=h_bank[:],
-                    lhsT=w1_q[:, span(t, P)].bitcast(FP8X4),
+                    lhsT=w1_q[t // 2][:, span(t % 2, P)].bitcast(FP8X4),
                     lhsT_scale=w1_s[:, span(t, P)],
                     rhs=xq[:, span(half, HALF)].bitcast(FP8X4),
                     rhs_scale=xs[:, span(half, HALF)],
@@ -151,7 +162,6 @@ def tile_picked_slorah_relu_po_kernel(
         z_s = [keep.tile([P, CHUNK], U8, name="z_s%d" % c, align_bytes=64) for c in range(CHUNKS)]
         y_halves = [keep.tile([P, PACK, HALF], F32, name="y%d" % half) for half in range(2)]
         y = [y_halves[c // 2][:, :, span(c % 2, CHUNK)] for c in range(CHUNKS)]
-        y_bf = keep.tile([P, S * PACK], BF16, name="y_bf", align_bytes=64)
         y_q = keep.tile([P, S], I32, name="y_q", align_bytes=64)
         y_s = keep.tile([P, S], U8, name="y_s", align_bytes=64)
         out_rows = out_0.rearrange("(p t) j -> p t j", t=PACK)
@@ -167,11 +177,11 @@ def tile_picked_slorah_relu_po_kernel(
             nc.tensor.matmul_mx(
                 out=banks[c][t // 2][:, t % 2, :],
                 lhsT=w_dealt[w][:, t, :].bitcast(FP4X4),
-                lhsT_scale=ws_dealt[:, w, t, :],
+                lhsT_scale=ws[:, span(w * PACK + t, P)],
                 rhs=codes.bitcast(FP8X4),
                 rhs_scale=scales,
-                start=(w == 0),
-                stop=(w == 1),
+                start=(w == 0 and t % 2 == 0),
+                stop=(w == 1 and t % 2 == 1),
             )
 
         def base_pass(c, t):
@@ -181,16 +191,18 @@ def tile_picked_slorah_relu_po_kernel(
             output_pass(1, c, t, z_q[c][:], z_s[c][:])
 
         for c in range(CHUNKS):
-            for u in range(2):
-                base_pass(c, 2 * u)
+            for t in range(PACK):
+                base_pass(c, t)
 
-        def finish_chunk(c, copy, woven):
-            planes = z[c // 2][:].rearrange("p (t n) -> p t n", t=PACK)
-            weave(copy, woven, planes[:, :, span(c % 2, CHUNK)])
-            quantise(z_q[c][:], z_s[c][:], woven)
+        z_bf = [keep.tile([P, CHUNK, PACK], BF16, name="z_bf%d" % c, align_bytes=64) for c in range(CHUNKS)]
+
+        def weave_z(c, copy):
+            weave(copy, z_bf[c][:], z[c // 2][:, :, span(c % 2, CHUNK)])
+
+        def finish_chunk(c):
+            quantise(z_q[c][:], z_s[c][:], z_bf[c][:])
             for u in range(2):
                 adapter_pass(c, 2 * u)
-                base_pass(c, 2 * u + 1)
                 adapter_pass(c, 2 * u + 1)
                 nc.scalar.copy(y[c][:, span(u, 2), :], banks[c][u][:])
                 if c < 2:
@@ -198,23 +210,31 @@ def tile_picked_slorah_relu_po_kernel(
                 elif c == CHUNKS - 1:
                     nc.sync.dma_start(out_rows[:, span(u, 2), span(1, HALF)], y_halves[1][:, span(u, 2), :])
 
-        finish_chunk(0, nc.scalar.copy, z_piece(2, 1).bitcast(BF16).rearrange("p (n t) -> p n t", t=PACK))
-        z_bf = keep.tile([P, CHUNK, PACK], BF16, name="z_bf", align_bytes=64)
-        finish_chunk(1, nc.scalar.copy, z_bf[:])
+        weave_z(0, nc.scalar.copy)
+        weave_z(1, nc.scalar.copy)
+        finish_chunk(0)
         gate(*pieces[-1])
-        z_bf = keep.tile([P, HALF, PACK], BF16, name="z_bf", align_bytes=64)
-        for c in range(CHUNKS // 2, CHUNKS):
-            finish_chunk(c, nc.vector.tensor_copy, z_bf[:, span(c % 2, CHUNK), :])
+        finish_chunk(1)
+        weave_z(2, nc.vector.tensor_copy)
+        weave_z(3, nc.vector.tensor_copy)
+        finish_chunk(2)
+        finish_chunk(3)
 
+        y_bf = keep.tile([P, S * PACK], BF16, name="z_bf3", align_bytes=64)
         y_woven = y_bf[:].rearrange("p (n t) -> p n t", t=PACK)
 
+        def weave_y(c):
+            weave(nc.vector.tensor_copy, y_woven[:, span(c, CHUNK), :], y[c])
+
         def quantise_y(first, count):
-            for c in range(first, first + count):
-                weave(nc.vector.tensor_copy, y_woven[:, span(c, CHUNK), :], y[c])
             cols = slice(first * CHUNK, (first + count) * CHUNK)
             quantise(y_q[:, cols], y_s[:, cols], y_woven[:, cols, :])
 
+        weave_y(0)
+        weave_y(1)
+        weave_y(2)
         quantise_y(0, 2)
+        weave_y(3)
         quantise_y(2, 1)
         nc.sync.dma_start(out_words[:, 0 : S - CHUNK], y_q[:, 0 : S - CHUNK])
         quantise_y(3, 1)

@@ -14,6 +14,7 @@ U8 = mybir.dt.uint8
 FP8X4 = mybir.dt.float8_e4m3fn_x4
 FP4X4 = mybir.dt.float4_e2m1fn_x4
 MULT = mybir.AluOpType.mult
+MAX = mybir.AluOpType.max
 RELU = mybir.ActivationFunctionType.Relu
 COPY = mybir.ActivationFunctionType.Copy
 
@@ -24,7 +25,6 @@ LIST_ROWS = 16
 HALF = S // 2
 CHUNK = 128
 CHUNKS = S // CHUNK
-X_FIRST = 7 * T // 16
 RUN = 2
 
 
@@ -53,7 +53,7 @@ def tile_picked_slorah_relu_po_kernel(
         xs = keep.tile([P, S], U8, name="xs", align_bytes=64)
         ws = keep.tile([P, 2 * N], U8, name="ws", align_bytes=64)
 
-        for tile in (xs_table, ws_raw, xs, ws):
+        for tile in (ws_raw, xs_table, xs, ws):
             nc.vector.memset(tile[:].bitcast(I32), 0)
 
         def move_scales(dst, src):
@@ -61,15 +61,15 @@ def tile_picked_slorah_relu_po_kernel(
                 nc.sync.dma_start(dst[scale_partitions(q), :].bitcast(I32), src[32 * q : 32 * q + 32 : 8, :].bitcast(I32))
 
         gain_rows = gain.rearrange("(p t) u -> p t u", t=PACK)
-        x_rows = x_words[0].rearrange("p n t -> p (n t)").bitcast(I32)
         nc.sync.dma_start(offs_sb[:], offs)
-        nc.sync.dma_start(x_table[:, 0:X_FIRST], x_rows[:, 0:X_FIRST])
+        nc.sync.dma_start(w_raw[0][:].bitcast(I32), w2_words[0].bitcast(I32))
+        nc.sync.dma_start(w_raw[1][:].bitcast(I32), w3_words[0].bitcast(I32))
         nc.sync.dma_start(ad_sb[:], ad)
-        nc.sync.dma_start(xs_table[0:P:8, :].bitcast(I32), x_scales[0].bitcast(I32))
         nc.sync.dma_start(ws_raw[0:P:8, span(0, N)].bitcast(I32), w2_scales[0].bitcast(I32))
         nc.sync.dma_start(ws_raw[0:P:8, span(1, N)].bitcast(I32), w3_scales[0].bitcast(I32))
+        nc.sync.dma_start(xs_table[0:P:8, :].bitcast(I32), x_scales[0].bitcast(I32))
         nc.sync.dma_start(w1_raw[:], w1.rearrange("(p j) c -> p j c", j=PACK))
-        nc.sync.dma_start(x_table[:, X_FIRST:T], x_rows[:, X_FIRST:T])
+        nc.sync.dma_start(x_table[:], x_words[0].rearrange("p n t -> p (n t)").bitcast(I32))
 
         w_dealt = [keep.tile([P, PACK, 2 * P], U8, name="w_dealt%d" % w, align_bytes=64) for w in range(2)]
 
@@ -79,15 +79,15 @@ def tile_picked_slorah_relu_po_kernel(
                 w_raw[w][:].bitcast(U16).rearrange("p (m t) -> p t m", t=PACK),
             )
 
+        deal_words(0)
+        deal_words(1)
         xs_picked = keep.tile([P, S], U8, name="xs_picked", align_bytes=64)
         nc.vector.tensor_copy(xs_picked[:], xs_table[:].indirect(offs_sb[:]))
         move_scales(xs, xs_picked)
-        nc.sync.dma_start(w_raw[0][:].bitcast(I32), w2_words[0].bitcast(I32))
-        nc.sync.dma_start(w_raw[1][:].bitcast(I32), w3_words[0].bitcast(I32))
 
         w1_pairs = w1_raw[:].rearrange("p j (m u e) -> p u m e j", u=2, e=2)
         w1_bf = [keep.tile([P, 2, P, PACK], BF16, name="w1_bf%d" % u, align_bytes=64) for u in range(2)]
-        w1_q = [keep.tile([P, 2 * P], U32, name="w1_q", align_bytes=64)]
+        w1_q = [keep.tile([P, 2 * P], U32, name="w1_q%d" % u, align_bytes=64) for u in range(2)]
         w1_s = keep.tile([P, PACK * P], U8, name="w1_s", align_bytes=64)
         nc.vector.tensor_copy(w1_bf[0][:].rearrange("p e m j -> p m e j"), w1_pairs[:, 0])
         nc.scalar.activation(w1_bf[1][:].rearrange("p e m j -> p m e j"), w1_pairs[:, 1], COPY)
@@ -105,8 +105,9 @@ def tile_picked_slorah_relu_po_kernel(
             ws_raw[:].rearrange("p (w m t) -> p w t m", w=2, t=PACK),
         )
         quantise_w1(0)
+        quantise_w1(1)
         for t in range(PACK):
-            if t == 2:
+            if t == 3:
                 move_scales(ws, ws_dealt)
             nc.sync.dma_start(gains[t][:], gain_rows[:, t, :])
 
@@ -116,10 +117,6 @@ def tile_picked_slorah_relu_po_kernel(
                 xq[:, span(half, HALF)].bitcast(U32),
                 x_table[:].bitcast(U32).indirect(offs_sb[:, span(half, HALF // LIST_ROWS)]),
             )
-        w1_q.append(keep.tile([P, 2 * P], U32, name="x_table", align_bytes=64))
-        deal_words(0)
-        quantise_w1(1)
-        deal_words(1)
 
         late_step = CHUNK + PACK * HALF
         early_start = 2 * late_step + CHUNK
@@ -220,7 +217,7 @@ def tile_picked_slorah_relu_po_kernel(
         finish_chunk(2)
         finish_chunk(3)
 
-        y_bf = keep.tile([P, S * PACK], BF16, name="z_bf3", align_bytes=64)
+        y_bf = keep.tile([P, S * PACK], BF16, name="y_bf", align_bytes=64)
         y_woven = y_bf[:].rearrange("p (n t) -> p n t", t=PACK)
 
         def weave_y(c):

@@ -45,7 +45,7 @@ def tile_picked_slorah_relu_po_kernel(
         offs_sb = keep.tile([P, S // LIST_ROWS], U16, name="offs_sb")
         ad_sb = keep.tile([P, S // LIST_ROWS], U16, name="ad_sb")
         x_table = keep.tile([P, T], I32, name="x_table", align_bytes=64)
-        xs_table = keep.tile([P, T], U8, name="xs_table")
+        xs_table = keep.tile([P, T], U8, name="xs_table", align_bytes=64)
         w_raw = [keep.tile([P, 2 * N], U8, name="w_raw%d" % w) for w in range(2)]
         ws_raw = keep.tile([P, 2 * N], U8, name="ws_raw")
         w1_raw = keep.tile([P, PACK, H], F32, name="w1_raw")
@@ -53,34 +53,35 @@ def tile_picked_slorah_relu_po_kernel(
         xs = keep.tile([P, S], U8, name="xs", align_bytes=64)
         ws = keep.tile([P, 2 * N], U8, name="ws", align_bytes=64)
 
-        for tile in (ws_raw, xs_table, xs, ws):
+        nc.gpsimd.memset(ws_raw[:].bitcast(I32), 0)
+        for tile in (xs_table, xs, ws):
             nc.vector.memset(tile[:].bitcast(I32), 0)
 
         def move_scales(dst, src):
-            for q in range(QUADRANTS):
-                nc.sync.dma_start(dst[scale_partitions(q), :].bitcast(I32), src[32 * q : 32 * q + 32 : 8, :].bitcast(I32))
+            for r in range(4):
+                nc.sync.dma_start(dst[r:P:32, :].bitcast(I32), src[8 * r : P : 32, :].bitcast(I32))
 
         gain_rows = gain.rearrange("(p t) u -> p t u", t=PACK)
         nc.sync.dma_start(offs_sb[:], offs)
-        nc.sync.dma_start(w_raw[0][:].bitcast(I32), w2_words[0].bitcast(I32))
-        nc.sync.dma_start(w_raw[1][:].bitcast(I32), w3_words[0].bitcast(I32))
+        nc.scalar.dma_start(w_raw[0][:].bitcast(I32), w2_words[0].bitcast(I32))
         nc.sync.dma_start(ad_sb[:], ad)
-        nc.sync.dma_start(ws_raw[0:P:8, span(0, N)].bitcast(I32), w2_scales[0].bitcast(I32))
-        nc.sync.dma_start(ws_raw[0:P:8, span(1, N)].bitcast(I32), w3_scales[0].bitcast(I32))
+        nc.scalar.dma_start(w_raw[1][:].bitcast(I32), w3_words[0].bitcast(I32))
         nc.sync.dma_start(xs_table[0:P:8, :].bitcast(I32), x_scales[0].bitcast(I32))
+        nc.scalar.dma_start(ws_raw[0:P:8, span(0, N)].bitcast(I32), w2_scales[0].bitcast(I32))
+        nc.scalar.dma_start(ws_raw[0:P:8, span(1, N)].bitcast(I32), w3_scales[0].bitcast(I32))
         nc.sync.dma_start(w1_raw[:], w1.rearrange("(p j) c -> p j c", j=PACK))
         nc.sync.dma_start(x_table[:], x_words[0].rearrange("p n t -> p (n t)").bitcast(I32))
 
-        w_dealt = [keep.tile([P, PACK, 2 * P], U8, name="w_dealt%d" % w, align_bytes=64) for w in range(2)]
+        w_dealt = []
 
-        def deal_words(w):
+        def deal_words(w, name):
+            w_dealt.append(keep.tile([P, PACK, 2 * P], U8, name=name, align_bytes=64))
             nc.vector.tensor_copy(
                 w_dealt[w][:].bitcast(U16),
                 w_raw[w][:].bitcast(U16).rearrange("p (m t) -> p t m", t=PACK),
             )
 
-        deal_words(0)
-        deal_words(1)
+        deal_words(0, "w2_dealt")
         xs_picked = keep.tile([P, S], U8, name="xs_picked", align_bytes=64)
         nc.vector.tensor_copy(xs_picked[:], xs_table[:].indirect(offs_sb[:]))
         move_scales(xs, xs_picked)
@@ -104,6 +105,7 @@ def tile_picked_slorah_relu_po_kernel(
             ws_dealt[:].rearrange("p (w t m) -> p w t m", w=2, t=PACK),
             ws_raw[:].rearrange("p (w m t) -> p w t m", w=2, t=PACK),
         )
+        deal_words(1, "xs_table")
         quantise_w1(0)
         quantise_w1(1)
         for t in range(PACK):

@@ -25,6 +25,7 @@ LIST_ROWS = 16
 HALF = S // 2
 CHUNK = 128
 CHUNKS = S // CHUNK
+ALIGN = 256
 RUN = 2
 
 
@@ -42,16 +43,16 @@ def tile_picked_slorah_relu_po_kernel(
     with ExitStack() as ctx:
         keep = ctx.enter_context(tc.tile_pool(name="keep", bufs=1))
 
-        offs_sb = keep.tile([P, S // LIST_ROWS], U16, name="offs_sb")
-        ad_sb = keep.tile([P, S // LIST_ROWS], U16, name="ad_sb")
-        x_table = keep.tile([P, T], I32, name="x_table", align_bytes=64)
-        xs_table = keep.tile([P, T], U8, name="xs_table", align_bytes=64)
-        w_raw = [keep.tile([P, 2 * N], U8, name="w_raw%d" % w) for w in range(2)]
-        ws_raw = keep.tile([P, 2 * N], U8, name="ws_raw")
-        w1_raw = keep.tile([P, PACK, H], F32, name="w1_raw")
-        gains = [keep.tile([P, U], F32, name="gain%d" % t) for t in range(PACK)]
-        xs = keep.tile([P, S], U8, name="xs", align_bytes=64)
-        ws = keep.tile([P, 2 * N], U8, name="ws", align_bytes=64)
+        offs_sb = keep.tile([P, S // LIST_ROWS], U16, name="offs_sb", align_bytes=ALIGN)
+        ad_sb = keep.tile([P, S // LIST_ROWS], U16, name="ad_sb", align_bytes=ALIGN)
+        x_table = keep.tile([P, T], I32, name="x_table", align_bytes=ALIGN)
+        xs_table = keep.tile([P, T], U8, name="xs_table", align_bytes=ALIGN)
+        w_raw = [keep.tile([P, 2 * N], U8, name="w_raw%d" % w, align_bytes=ALIGN) for w in range(2)]
+        ws_raw = keep.tile([P, 2 * N], U8, name="ws_raw", align_bytes=ALIGN)
+        w1_raw = keep.tile([P, PACK, H], F32, name="w1_raw", align_bytes=ALIGN)
+        gains = [keep.tile([P, U], F32, name="gain%d" % t, align_bytes=ALIGN) for t in range(PACK)]
+        xs = keep.tile([P, S], U8, name="xs", align_bytes=ALIGN)
+        ws = keep.tile([P, 2 * N], U8, name="ws", align_bytes=ALIGN)
 
         nc.gpsimd.memset(ws_raw[:].bitcast(I32), 0)
         for tile in (xs_table, xs, ws):
@@ -75,21 +76,21 @@ def tile_picked_slorah_relu_po_kernel(
         w_dealt = []
 
         def deal_words(w, name):
-            w_dealt.append(keep.tile([P, PACK, 2 * P], U8, name=name, align_bytes=64))
+            w_dealt.append(keep.tile([P, PACK, 2 * P], U8, name=name, align_bytes=ALIGN))
             nc.vector.tensor_copy(
                 w_dealt[w][:].bitcast(U16),
                 w_raw[w][:].bitcast(U16).rearrange("p (m t) -> p t m", t=PACK),
             )
 
         deal_words(0, "w2_dealt")
-        xs_picked = keep.tile([P, S], U8, name="xs_picked", align_bytes=64)
+        xs_picked = keep.tile([P, S], U8, name="xs_picked", align_bytes=ALIGN)
         nc.vector.tensor_copy(xs_picked[:], xs_table[:].indirect(offs_sb[:]))
         move_scales(xs, xs_picked)
 
         w1_pairs = w1_raw[:].rearrange("p j (m u e) -> p u m e j", u=2, e=2)
-        w1_bf = [keep.tile([P, 2, P, PACK], BF16, name="w1_bf%d" % u, align_bytes=64) for u in range(2)]
-        w1_q = [keep.tile([P, 2 * P], U32, name="w1_q%d" % u, align_bytes=64) for u in range(2)]
-        w1_s = keep.tile([P, PACK * P], U8, name="w1_s", align_bytes=64)
+        w1_bf = [keep.tile([P, 2, P, PACK], BF16, name="w1_bf%d" % u, align_bytes=ALIGN) for u in range(2)]
+        w1_q = [keep.tile([P, 2 * P], U32, name="w1_q%d" % u, align_bytes=ALIGN) for u in range(2)]
+        w1_s = keep.tile([P, PACK * P], U8, name="w1_s", align_bytes=ALIGN)
         nc.vector.tensor_copy(w1_bf[0][:].rearrange("p e m j -> p m e j"), w1_pairs[:, 0])
         nc.scalar.activation(w1_bf[1][:].rearrange("p e m j -> p m e j"), w1_pairs[:, 1], COPY)
 
@@ -100,7 +101,7 @@ def tile_picked_slorah_relu_po_kernel(
                 in_=w1_bf[u][:].rearrange("p e m j -> p (e m j)"),
             )
 
-        ws_dealt = keep.tile([P, 2 * N], U8, name="ws_dealt")
+        ws_dealt = keep.tile([P, 2 * N], U8, name="ws_dealt", align_bytes=ALIGN)
         nc.vector.tensor_copy(
             ws_dealt[:].rearrange("p (w t m) -> p w t m", w=2, t=PACK),
             ws_raw[:].rearrange("p (w m t) -> p w t m", w=2, t=PACK),
@@ -113,7 +114,7 @@ def tile_picked_slorah_relu_po_kernel(
                 move_scales(ws, ws_dealt)
             nc.sync.dma_start(gains[t][:], gain_rows[:, t, :])
 
-        xq = keep.tile([P, S], I32, name="xq", align_bytes=64)
+        xq = keep.tile([P, S], I32, name="xq", align_bytes=ALIGN)
         for half in range(2):
             nc.vector.tensor_copy(
                 xq[:, span(half, HALF)].bitcast(U32),
@@ -122,7 +123,7 @@ def tile_picked_slorah_relu_po_kernel(
 
         late_step = CHUNK + PACK * HALF
         early_start = 2 * late_step + CHUNK
-        z_tile = keep.tile([P, PACK * late_step], F32, name="z", align_bytes=64)
+        z_tile = keep.tile([P, PACK * late_step], F32, name="z", align_bytes=ALIGN)
         early = z_tile[:, early_start : early_start + PACK * HALF].rearrange("p (t n) -> p t n", t=PACK)
         late = z_tile[:].rearrange("p (t n) -> p t n", t=PACK)[:, :, 0:HALF]
         z = [early, late]
@@ -135,7 +136,7 @@ def tile_picked_slorah_relu_po_kernel(
         with tc.psum_pool(name="h_psum", bufs=3) as h_psum:
             for t, half in pieces:
                 if (t, half) not in h:
-                    h[t, half] = keep.tile([P, HALF], F32, name="h%d%d" % (t, half))[:]
+                    h[t, half] = keep.tile([P, HALF], F32, name="h%d%d" % (t, half), align_bytes=ALIGN)[:]
                 h_bank = h_psum.tile([P, HALF], F32, name="h_bank")
                 nc.tensor.matmul_mx(
                     out=h_bank[:],
@@ -157,12 +158,12 @@ def tile_picked_slorah_relu_po_kernel(
 
         y_psum = ctx.enter_context(tc.psum_pool(name="y_psum", bufs=1))
         banks = [[y_psum.tile([P, 2, CHUNK], F32, name="y_bank%d%d" % (c, u)) for u in range(2)] for c in range(CHUNKS)]
-        z_q = [keep.tile([P, CHUNK], U32, name="z_q%d" % c, align_bytes=64) for c in range(CHUNKS)]
-        z_s = [keep.tile([P, CHUNK], U8, name="z_s%d" % c, align_bytes=64) for c in range(CHUNKS)]
-        y_halves = [keep.tile([P, PACK, HALF], F32, name="y%d" % half) for half in range(2)]
+        z_q = [keep.tile([P, CHUNK], U32, name="z_q%d" % c, align_bytes=ALIGN) for c in range(CHUNKS)]
+        z_s = [keep.tile([P, CHUNK], U8, name="z_s%d" % c, align_bytes=ALIGN) for c in range(CHUNKS)]
+        y_halves = [keep.tile([P, PACK, HALF], F32, name="y%d" % half, align_bytes=ALIGN) for half in range(2)]
         y = [y_halves[c // 2][:, :, span(c % 2, CHUNK)] for c in range(CHUNKS)]
-        y_q = keep.tile([P, S], I32, name="y_q", align_bytes=64)
-        y_s = keep.tile([P, S], U8, name="y_s", align_bytes=64)
+        y_q = keep.tile([P, S], I32, name="y_q", align_bytes=ALIGN)
+        y_s = keep.tile([P, S], U8, name="y_s", align_bytes=ALIGN)
         out_rows = out_0.rearrange("(p t) j -> p t j", t=PACK)
         out_words = out_1[0].rearrange("p n t -> p (n t)").bitcast(I32)
 
@@ -193,7 +194,7 @@ def tile_picked_slorah_relu_po_kernel(
             for t in range(PACK):
                 base_pass(c, t)
 
-        z_bf = [keep.tile([P, CHUNK, PACK], BF16, name="z_bf%d" % c, align_bytes=64) for c in range(CHUNKS)]
+        z_bf = [keep.tile([P, CHUNK, PACK], BF16, name="z_bf%d" % c, align_bytes=ALIGN) for c in range(CHUNKS)]
 
         def weave_z(c, copy):
             weave(copy, z_bf[c][:], z[c // 2][:, :, span(c % 2, CHUNK)])
@@ -219,7 +220,7 @@ def tile_picked_slorah_relu_po_kernel(
         finish_chunk(2)
         finish_chunk(3)
 
-        y_bf = keep.tile([P, S * PACK], BF16, name="y_bf", align_bytes=64)
+        y_bf = keep.tile([P, S * PACK], BF16, name="y_bf", align_bytes=ALIGN)
         y_woven = y_bf[:].rearrange("p (n t) -> p n t", t=PACK)
 
         def weave_y(c):

@@ -131,33 +131,42 @@ def tile_picked_slorah_relu_po_kernel(
         def z_piece(t, half):
             return z[half][:, t, :]
 
-        pieces = [(0, 0), (0, 1), (1, 0), (2, 0), (3, 0), (3, 1), (1, 1), (2, 1)]
-        h = {(3, 0): z_piece(1, 1)}
-        with tc.psum_pool(name="h_psum", bufs=3) as h_psum:
-            for t, half in pieces:
-                if (t, half) not in h:
-                    h[t, half] = keep.tile([P, HALF], F32, name="h%d%d" % (t, half), align_bytes=ALIGN)[:]
-                h_bank = h_psum.tile([P, HALF], F32, name="h_bank")
-                nc.tensor.matmul_mx(
-                    out=h_bank[:],
-                    lhsT=w1_q[t // 2][:, span(t % 2, P)].bitcast(FP8X4),
-                    lhsT_scale=w1_s[:, span(t, P)],
-                    rhs=xq[:, span(half, HALF)].bitcast(FP8X4),
-                    rhs_scale=xs[:, span(half, HALF)],
-                    start=True,
-                    stop=True,
-                )
-                nc.scalar.activation(h[t, half], h_bank[:], RELU)
+        psum = ctx.enter_context(tc.psum_pool(name="psum", bufs=1))
+        picked = keep.tile([P, 2, HALF], F32, name="picked", align_bytes=ALIGN)
+        fused = [(0, 0), (0, 1), (1, 0), (2, 0), (3, 0), (3, 1)]
+        h = {}
 
-        def gate(t, half):
-            entries = ad_sb[:, span(half, HALF // LIST_ROWS)]
-            nc.vector.tensor_tensor(z_piece(t, half), gains[t][:].indirect(entries), h[t, half], MULT)
+        def hidden(t, half, h_bank):
+            nc.tensor.matmul_mx(
+                out=h_bank,
+                lhsT=w1_q[t // 2][:, span(t % 2, P)].bitcast(FP8X4),
+                lhsT_scale=w1_s[:, span(t, P)],
+                rhs=xq[:, span(half, HALF)].bitcast(FP8X4),
+                rhs_scale=xs[:, span(half, HALF)],
+                start=True,
+                stop=True,
+            )
 
-        for t, half in pieces[:-1]:
+        for i, (t, half) in enumerate(fused):
+            h[t, half] = keep.tile([P, HALF], F32, name="h%d%d" % (t, half), align_bytes=ALIGN)
+            h_bank = psum.tile([P, HALF], F32, name="bank%d" % i)
+            hidden(t, half, h_bank[:])
+            nc.scalar.activation(h[t, half][:], h_bank[:], RELU)
+        held = psum.tile([P, 2, HALF], F32, name="bank5")
+        for t in (1, 2):
+            hidden(t, 1, held[:, t - 1, :])
+            window = gains[t][:].indirect(ad_sb[:, span(1, HALF // LIST_ROWS)])
+            nc.scalar.activation(picked[:, t - 1, :], window, COPY)
+
+        def gate(t, half, part=slice(0, HALF)):
+            entries = ad_sb[:, (half * HALF + part.start) // LIST_ROWS : (half * HALF + part.stop) // LIST_ROWS]
+            nc.vector.tensor_tensor(z_piece(t, half)[:, part], gains[t][:].indirect(entries), h[t, half][:, part], MULT)
+
+        for t, half in fused[:4]:
             gate(t, half)
 
-        y_psum = ctx.enter_context(tc.psum_pool(name="y_psum", bufs=1))
-        banks = [[y_psum.tile([P, 2, CHUNK], F32, name="y_bank%d%d" % (c, u)) for u in range(2)] for c in range(CHUNKS)]
+        taken = [[6, 0], [1, 2], [3, 4], [7, 5]]
+        banks = [[None, None] for c in range(CHUNKS)]
         z_q = [keep.tile([P, CHUNK], U32, name="z_q%d" % c, align_bytes=ALIGN) for c in range(CHUNKS)]
         z_s = [keep.tile([P, CHUNK], U8, name="z_s%d" % c, align_bytes=ALIGN) for c in range(CHUNKS)]
         y_halves = [keep.tile([P, PACK, HALF], F32, name="y%d" % half, align_bytes=ALIGN) for half in range(2)]
@@ -190,9 +199,15 @@ def tile_picked_slorah_relu_po_kernel(
         def adapter_pass(c, t):
             output_pass(1, c, t, z_q[c][:], z_s[c][:])
 
+        def open_bank(c, u):
+            banks[c][u] = psum.tile([P, 2, CHUNK], F32, name="bank%d" % taken[c][u])
+            base_pass(c, 2 * u)
+            base_pass(c, 2 * u + 1)
+
         for c in range(CHUNKS):
-            for t in range(PACK):
-                base_pass(c, t)
+            for u in range(2):
+                if taken[c][u] != 5:
+                    open_bank(c, u)
 
         z_bf = [keep.tile([P, CHUNK, PACK], BF16, name="z_bf%d" % c, align_bytes=ALIGN) for c in range(CHUNKS)]
 
@@ -210,10 +225,16 @@ def tile_picked_slorah_relu_po_kernel(
                 elif c == CHUNKS - 1:
                     nc.sync.dma_start(out_rows[:, span(u, 2), span(1, HALF)], y_halves[1][:, span(u, 2), :])
 
+        gate(3, 0, span(0, CHUNK))
         weave_z(0, nc.scalar.copy)
+        gate(3, 0, span(1, CHUNK))
         weave_z(1, nc.scalar.copy)
+        gate(3, 1)
         finish_chunk(0)
-        gate(*pieces[-1])
+        nc.vector.scalar_tensor_tensor(
+            out=late[:, 1:3, :], in0=held[:], scalar=0.0, in1=picked[:], op0=MAX, op1=MULT
+        )
+        open_bank(3, 1)
         finish_chunk(1)
         weave_z(2, nc.vector.tensor_copy)
         weave_z(3, nc.vector.tensor_copy)

@@ -26,7 +26,7 @@ HALF = S // 2
 CHUNK = 128
 CHUNKS = S // CHUNK
 ALIGN = 256
-RUN = 2
+RUN = 4
 
 
 def tile_picked_slorah_relu_po_kernel(

@@ -115,62 +115,76 @@ def tile_picked_slorah_relu_po_kernel(
             nc.sync.dma_start(gains[t][:], gain_rows[:, t, :])
 
         xq = keep.tile([P, S], I32, name="xq", align_bytes=ALIGN)
-        for half in range(2):
-            nc.vector.tensor_copy(
-                xq[:, span(half, HALF)].bitcast(U32),
-                x_table[:].bitcast(U32).indirect(offs_sb[:, span(half, HALF // LIST_ROWS)]),
-            )
 
-        late_step = CHUNK + PACK * HALF
-        early_start = 2 * late_step + CHUNK
-        z_tile = keep.tile([P, PACK * late_step], F32, name="z", align_bytes=ALIGN)
-        early = z_tile[:, early_start : early_start + PACK * HALF].rearrange("p (t n) -> p t n", t=PACK)
-        late = z_tile[:].rearrange("p (t n) -> p t n", t=PACK)[:, :, 0:HALF]
-        z = [early, late]
+        def entries(lists, cols):
+            return lists[:, cols.start // LIST_ROWS : cols.stop // LIST_ROWS]
 
-        def z_piece(t, half):
-            return z[half][:, t, :]
+        chunks = [span(c, CHUNK) for c in range(CHUNKS)]
+        halves = [span(half, HALF) for half in range(2)]
+        inner = slice(CHUNK, CHUNK + HALF)
+        outer = (0, CHUNKS - 1)
+        for cols in (chunks[0], chunks[3], inner):
+            nc.vector.tensor_copy(xq[:, cols].bitcast(U32), x_table[:].bitcast(U32).indirect(entries(offs_sb, cols)))
 
         psum = ctx.enter_context(tc.psum_pool(name="psum", bufs=1))
-        picked = keep.tile([P, 2, HALF], F32, name="picked", align_bytes=ALIGN)
-        fused = [(0, 0), (0, 1), (1, 0), (2, 0), (3, 0), (3, 1)]
-        h = {}
 
-        def hidden(t, half, h_bank):
+        def hidden(t, cols, h_bank):
             nc.tensor.matmul_mx(
                 out=h_bank,
                 lhsT=w1_q[t // 2][:, span(t % 2, P)].bitcast(FP8X4),
                 lhsT_scale=w1_s[:, span(t, P)],
-                rhs=xq[:, span(half, HALF)].bitcast(FP8X4),
-                rhs_scale=xs[:, span(half, HALF)],
+                rhs=xq[:, cols].bitcast(FP8X4),
+                rhs_scale=xs[:, cols],
                 start=True,
                 stop=True,
             )
 
-        for i, (t, half) in enumerate(fused):
-            h[t, half] = keep.tile([P, HALF], F32, name="h%d%d" % (t, half), align_bytes=ALIGN)
-            h_bank = psum.tile([P, HALF], F32, name="bank%d" % i)
-            hidden(t, half, h_bank[:])
-            nc.scalar.activation(h[t, half][:], h_bank[:], RELU)
-        held = psum.tile([P, 2, HALF], F32, name="bank5")
-        for t in (1, 2):
-            hidden(t, 1, held[:, t - 1, :])
-            window = gains[t][:].indirect(ad_sb[:, span(1, HALF // LIST_ROWS)])
-            nc.scalar.activation(picked[:, t - 1, :], window, COPY)
+        h = {}
+        for bank, planes in enumerate([[0], [1], [2, 3]]):
+            h_bank = psum.tile([P, len(planes), HALF], F32, name="bank%d" % bank)
+            h_sb = keep.tile([P, len(planes), HALF], F32, name="h%d" % bank, align_bytes=ALIGN)
+            for slot, t in enumerate(planes):
+                for i, c in enumerate(outer):
+                    hidden(t, chunks[c], h_bank[:, slot, chunks[i]])
+                h[t] = h_sb[:, slot, :]
+            nc.scalar.activation(h_sb[:], h_bank[:], RELU)
+        held = {}
+        for c, bank in ((1, 3), (2, 2)):
+            held[c] = psum.tile([P, PACK, CHUNK], F32, name="bank%d" % bank)
+            for t in range(PACK):
+                hidden(t, chunks[c], held[c][:, t, :])
 
-        def gate(t, half, part=slice(0, HALF)):
-            entries = ad_sb[:, (half * HALF + part.start) // LIST_ROWS : (half * HALF + part.stop) // LIST_ROWS]
-            nc.vector.tensor_tensor(z_piece(t, half)[:, part], gains[t][:].indirect(entries), h[t, half][:, part], MULT)
+        z_tile = keep.tile([P, CHUNK + PACK * HALF], F32, name="z", align_bytes=ALIGN)
+        z = z_tile[:, CHUNK:].rearrange("p (t n) -> p t n", t=PACK)
+        picked = keep.tile([P, PACK, HALF], F32, name="picked", align_bytes=ALIGN)
 
-        for t, half in fused[:4]:
-            gate(t, half)
+        def inner_window(t):
+            return gains[t][:].indirect(entries(ad_sb, inner))
 
-        taken = [[6, 0], [1, 2], [3, 4], [7, 5]]
-        banks = [[None, None] for c in range(CHUNKS)]
+        def gate(t, c):
+            part = chunks[outer.index(c)]
+            window = gains[t][:].indirect(entries(ad_sb, chunks[c]))
+            nc.vector.tensor_tensor(z[:, t, part], window, h[t][:, part], MULT)
+
+        nc.vector.tensor_copy(picked[:, 0, :], inner_window(0))
+        for t in range(PACK - 1):
+            for c in outer:
+                gate(t, c)
+        for t in range(1, PACK):
+            nc.scalar.activation(picked[:, t, :], inner_window(t), COPY)
+
+        order = [0, 1, 3, 2]
+        taken = {0: [4, 5], 1: [6, 7], 3: [0, 1], 2: [3, 2]}
+        banks = {c: [None, None] for c in order}
+        z_bf = {c: keep.tile([P, CHUNK, PACK], BF16, name="z_bf%d" % c, align_bytes=ALIGN)[:] for c in (0, 1)}
+        z_bf[2] = z_tile[:, : 2 * CHUNK].bitcast(BF16).rearrange("p (n t) -> p n t", t=PACK)
         z_q = [keep.tile([P, CHUNK], U32, name="z_q%d" % c, align_bytes=ALIGN) for c in range(CHUNKS)]
         z_s = [keep.tile([P, CHUNK], U8, name="z_s%d" % c, align_bytes=ALIGN) for c in range(CHUNKS)]
         y_halves = [keep.tile([P, PACK, HALF], F32, name="y%d" % half, align_bytes=ALIGN) for half in range(2)]
-        y = [y_halves[c // 2][:, :, span(c % 2, CHUNK)] for c in range(CHUNKS)]
+        y = [y_halves[c // 2][:, :, chunks[c % 2]] for c in range(CHUNKS)]
+        z_bf[3] = y_halves[0][:, PACK - 1, :].bitcast(BF16).rearrange("p (n t) -> p n t", t=PACK)
+        y_bf = keep.tile([P, S * PACK], BF16, name="y_bf", align_bytes=ALIGN)
+        y_woven = y_bf[:].rearrange("p (n t) -> p n t", t=PACK)
         y_q = keep.tile([P, S], I32, name="y_q", align_bytes=ALIGN)
         y_s = keep.tile([P, S], U8, name="y_s", align_bytes=ALIGN)
         out_rows = out_0.rearrange("(p t) j -> p t j", t=PACK)
@@ -193,73 +207,73 @@ def tile_picked_slorah_relu_po_kernel(
                 stop=(w == 1 and t % 2 == 1),
             )
 
-        def base_pass(c, t):
-            output_pass(0, c, t, xq[:, span(c, CHUNK)], xs[:, span(c, CHUNK)])
-
-        def adapter_pass(c, t):
-            output_pass(1, c, t, z_q[c][:], z_s[c][:])
-
         def open_bank(c, u):
             banks[c][u] = psum.tile([P, 2, CHUNK], F32, name="bank%d" % taken[c][u])
-            base_pass(c, 2 * u)
-            base_pass(c, 2 * u + 1)
+            for t in (2 * u, 2 * u + 1):
+                output_pass(0, c, t, xq[:, chunks[c]], xs[:, chunks[c]])
 
-        for c in range(CHUNKS):
+        for c in order[:-1]:
             for u in range(2):
-                if taken[c][u] != 5:
-                    open_bank(c, u)
+                open_bank(c, u)
 
-        z_bf = [keep.tile([P, CHUNK, PACK], BF16, name="z_bf%d" % c, align_bytes=ALIGN) for c in range(CHUNKS)]
+        def weave_z(c):
+            weave(nc.scalar.copy, z_bf[c], z[:, :, chunks[outer.index(c)]])
 
-        def weave_z(c, copy):
-            weave(copy, z_bf[c][:], z[c // 2][:, :, span(c % 2, CHUNK)])
+        def gate_and_weave(c):
+            nc.vector.scalar_tensor_tensor(
+                out=z_bf[c],
+                in0=held[c][:].rearrange("p t n -> p n t"),
+                scalar=0.0,
+                in1=picked[:, :, chunks[c - 1]].rearrange("p t n -> p n t"),
+                op0=MAX,
+                op1=MULT,
+            )
 
-        def finish_chunk(c):
-            quantise(z_q[c][:], z_s[c][:], z_bf[c][:])
-            for u in range(2):
-                adapter_pass(c, 2 * u)
-                adapter_pass(c, 2 * u + 1)
-                nc.scalar.copy(y[c][:, span(u, 2), :], banks[c][u][:])
-                if c < 2:
-                    nc.sync.dma_start(out_rows[:, span(u, 2), span(c, CHUNK)], y[c][:, span(u, 2), :])
-                elif c == CHUNKS - 1:
-                    nc.sync.dma_start(out_rows[:, span(u, 2), span(1, HALF)], y_halves[1][:, span(u, 2), :])
+        def adapter(c):
+            quantise(z_q[c][:], z_s[c][:], z_bf[c])
+            for t in range(PACK):
+                output_pass(1, c, t, z_q[c][:], z_s[c][:])
 
-        gate(3, 0, span(0, CHUNK))
-        weave_z(0, nc.scalar.copy)
-        gate(3, 0, span(1, CHUNK))
-        weave_z(1, nc.scalar.copy)
-        gate(3, 1)
-        finish_chunk(0)
-        nc.vector.scalar_tensor_tensor(
-            out=late[:, 1:3, :], in0=held[:], scalar=0.0, in1=picked[:], op0=MAX, op1=MULT
-        )
-        open_bank(3, 1)
-        finish_chunk(1)
-        weave_z(2, nc.vector.tensor_copy)
-        weave_z(3, nc.vector.tensor_copy)
-        finish_chunk(2)
-        finish_chunk(3)
+        def empty_bank(c, u, copy):
+            copy(y[c][:, span(u, 2), :], banks[c][u][:])
 
-        y_bf = keep.tile([P, S * PACK], BF16, name="y_bf", align_bytes=ALIGN)
-        y_woven = y_bf[:].rearrange("p (n t) -> p n t", t=PACK)
+        def store_rows(half, u):
+            nc.sync.dma_start(out_rows[:, span(u, 2), halves[half]], y_halves[half][:, span(u, 2), :])
 
         def weave_y(c):
-            weave(nc.vector.tensor_copy, y_woven[:, span(c, CHUNK), :], y[c])
+            weave(nc.vector.tensor_copy, y_woven[:, chunks[c], :], y[c])
 
-        def quantise_y(first, count):
-            cols = slice(first * CHUNK, (first + count) * CHUNK)
-            quantise(y_q[:, cols], y_s[:, cols], y_woven[:, cols, :])
+        def quantise_y(c):
+            quantise(y_q[:, chunks[c]], y_s[:, chunks[c]], y_woven[:, chunks[c], :])
 
-        weave_y(0)
-        weave_y(1)
-        weave_y(2)
-        quantise_y(0, 2)
-        weave_y(3)
-        quantise_y(2, 1)
-        nc.sync.dma_start(out_words[:, 0 : S - CHUNK], y_q[:, 0 : S - CHUNK])
-        quantise_y(3, 1)
-        nc.sync.dma_start(out_words[:, S - CHUNK : S], y_q[:, S - CHUNK : S])
+        gate(3, 0)
+        weave_z(0)
+        gate(3, 3)
+        weave_z(3)
+        gate_and_weave(1)
+        open_bank(2, 0)
+        adapter(0)
+        adapter(1)
+        gate_and_weave(2)
+        open_bank(2, 1)
+        adapter(3)
+        adapter(2)
+        empty_bank(0, 0, nc.scalar.copy)
+        empty_bank(1, 0, nc.scalar.copy)
+        store_rows(0, 0)
+        empty_bank(0, 1, nc.scalar.copy)
+        empty_bank(1, 1, nc.vector.tensor_copy)
+        store_rows(0, 1)
+        for u in range(2):
+            empty_bank(3, u, nc.scalar.copy)
+            empty_bank(2, u, nc.scalar.copy)
+            store_rows(1, u)
+        for half in range(2):
+            weave_y(2 * half)
+            weave_y(2 * half + 1)
+            quantise_y(2 * half)
+            quantise_y(2 * half + 1)
+            nc.sync.dma_start(out_words[:, halves[half]], y_q[:, halves[half]])
         for q in range(QUADRANTS):
             queue = nc.scalar if q % 2 == 0 else nc.sync
             queue.dma_start(out_2[0, span(q, 4), :].bitcast(I32), y_s[scale_partitions(q), :].bitcast(I32))

@@ -140,14 +140,18 @@ def tile_picked_slorah_relu_po_kernel(
             )
 
         h = {}
-        for bank, planes in enumerate([[0], [1], [2, 3]]):
-            h_bank = psum.tile([P, len(planes), HALF], F32, name="bank%d" % bank)
-            h_sb = keep.tile([P, len(planes), HALF], F32, name="h%d" % bank, align_bytes=ALIGN)
-            for slot, t in enumerate(planes):
-                for i, c in enumerate(outer):
-                    hidden(t, chunks[c], h_bank[:, slot, chunks[i]])
-                h[t] = h_sb[:, slot, :]
-            nc.scalar.activation(h_sb[:], h_bank[:], RELU)
+        pieces = [(t, c) for t in range(PACK) for c in outer]
+        for bank, groups in enumerate([[pieces[0:2]], [pieces[2:5]], [pieces[5:8]]]):
+            h_bank = psum.tile([P, 3, CHUNK], F32, name="bank%d" % bank)
+            for slot, (t, c) in enumerate(sum(groups, [])):
+                hidden(t, chunks[c], h_bank[:, slot, :])
+            first = 0
+            for group in groups:
+                h_sb = keep.tile([P, len(group), CHUNK], F32, name="h%d%d" % group[0], align_bytes=ALIGN)
+                nc.scalar.activation(h_sb[:], h_bank[:, first : first + len(group), :], RELU)
+                for slot, piece in enumerate(group):
+                    h[piece] = h_sb[:, slot, :]
+                first = first + len(group)
         held = {}
         for c, bank in ((1, 3), (2, 2)):
             held[c] = psum.tile([P, PACK, CHUNK], F32, name="bank%d" % bank)
@@ -164,7 +168,7 @@ def tile_picked_slorah_relu_po_kernel(
         def gate(t, c):
             part = chunks[outer.index(c)]
             window = gains[t][:].indirect(entries(ad_sb, chunks[c]))
-            nc.vector.tensor_tensor(z[:, t, part], window, h[t][:, part], MULT)
+            nc.vector.tensor_tensor(z[:, t, part], window, h[t, c], MULT)
 
         nc.vector.tensor_copy(picked[:, 0, :], inner_window(0))
         for t in range(PACK - 1):
@@ -176,8 +180,7 @@ def tile_picked_slorah_relu_po_kernel(
         order = [0, 1, 3, 2]
         taken = {0: [4, 5], 1: [6, 7], 3: [0, 1], 2: [3, 2]}
         banks = {c: [None, None] for c in order}
-        z_bf = {c: keep.tile([P, CHUNK, PACK], BF16, name="z_bf%d" % c, align_bytes=ALIGN)[:] for c in (0, 1)}
-        z_bf[2] = z_tile[:, : 2 * CHUNK].bitcast(BF16).rearrange("p (n t) -> p n t", t=PACK)
+        z_bf = {0: keep.tile([P, CHUNK, PACK], BF16, name="z_bf0", align_bytes=ALIGN)[:]}
         z_q = [keep.tile([P, CHUNK], U32, name="z_q%d" % c, align_bytes=ALIGN) for c in range(CHUNKS)]
         z_s = [keep.tile([P, CHUNK], U8, name="z_s%d" % c, align_bytes=ALIGN) for c in range(CHUNKS)]
         y_halves = [keep.tile([P, PACK, HALF], F32, name="y%d" % half, align_bytes=ALIGN) for half in range(2)]
@@ -216,15 +219,16 @@ def tile_picked_slorah_relu_po_kernel(
             for u in range(2):
                 open_bank(c, u)
 
-        def weave_z(c):
-            weave(nc.scalar.copy, z_bf[c], z[:, :, chunks[outer.index(c)]])
+        def weave_z(c, copy, start, stop):
+            first = outer.index(c) * CHUNK
+            weave(copy, z_bf[c][:, start:stop, :], z[:, :, first + start : first + stop])
 
-        def gate_and_weave(c):
+        def gate_and_weave(c, planes):
             nc.vector.scalar_tensor_tensor(
-                out=z_bf[c],
-                in0=held[c][:].rearrange("p t n -> p n t"),
+                out=z_bf[c][:, :, planes],
+                in0=held[c][:, planes, :].rearrange("p t n -> p n t"),
                 scalar=0.0,
-                in1=picked[:, :, chunks[c - 1]].rearrange("p t n -> p n t"),
+                in1=picked[:, planes, chunks[c - 1]].rearrange("p t n -> p n t"),
                 op0=MAX,
                 op1=MULT,
             )
@@ -246,15 +250,19 @@ def tile_picked_slorah_relu_po_kernel(
         def quantise_y(c):
             quantise(y_q[:, chunks[c]], y_s[:, chunks[c]], y_woven[:, chunks[c], :])
 
+        z_bf[1] = keep.tile([P, CHUNK, PACK], BF16, name="h10", align_bytes=ALIGN)[:]
+        gate_and_weave(1, span(0, 2))
         gate(3, 0)
-        weave_z(0)
+        weave_z(0, nc.scalar.copy, 0, CHUNK // 2)
         gate(3, 3)
-        weave_z(3)
-        gate_and_weave(1)
+        weave_z(0, nc.vector.tensor_copy, CHUNK // 2, CHUNK)
+        weave_z(3, nc.scalar.copy, 0, CHUNK)
+        z_bf[2] = z_tile[:, : 2 * CHUNK].bitcast(BF16).rearrange("p (n t) -> p n t", t=PACK)
+        gate_and_weave(1, span(1, 2))
         open_bank(2, 0)
         adapter(0)
         adapter(1)
-        gate_and_weave(2)
+        gate_and_weave(2, span(0, PACK))
         open_bank(2, 1)
         adapter(3)
         adapter(2)
@@ -275,5 +283,4 @@ def tile_picked_slorah_relu_po_kernel(
             quantise_y(2 * half + 1)
             nc.sync.dma_start(out_words[:, halves[half]], y_q[:, halves[half]])
         for q in range(QUADRANTS):
-            queue = nc.scalar if q % 2 == 0 else nc.sync
-            queue.dma_start(out_2[0, span(q, 4), :].bitcast(I32), y_s[scale_partitions(q), :].bitcast(I32))
+            nc.sync.dma_start(out_2[0, span(q, 4), :].bitcast(I32), y_s[scale_partitions(q), :].bitcast(I32))

from contextlib import ExitStack

import concourse.mybir as mybir

K, T, S, N, H, U = 512, 2048, 512, 512, 512, 1024
FLOPS = 2 * S * (K * H + K * N + H * N)

F32 = mybir.dt.float32
BF16 = mybir.dt.bfloat16
I32 = mybir.dt.int32
U32 = mybir.dt.uint32
U16 = mybir.dt.uint16
U8 = mybir.dt.uint8
FP8X4 = mybir.dt.float8_e4m3fn_x4
FP4X4 = mybir.dt.float4_e2m1fn_x4
MULT = mybir.AluOpType.mult
MAX = mybir.AluOpType.max
RELU = mybir.ActivationFunctionType.Relu
COPY = mybir.ActivationFunctionType.Copy

P = 128
PACK = 4
QUADRANTS = 4
LIST_ROWS = 16
HALF = S // 2
CHUNK = 128
CHUNKS = S // CHUNK
ALIGN = 256
RUN = 4


def tile_picked_slorah_relu_po_kernel(
    tc, x_words, x_scales, w1, gain, w2_words, w2_scales, w3_words, w3_scales, offs, ad, out_0, out_1, out_2
):
    nc = tc.nc

    def span(i, width):
        return slice(i * width, (i + 1) * width)

    def scale_partitions(q):
        return slice(32 * q, 32 * q + 4)

    with ExitStack() as ctx:
        keep = ctx.enter_context(tc.tile_pool(name="keep", bufs=1))

        offs_sb = keep.tile([P, S // LIST_ROWS], U16, name="offs_sb", align_bytes=ALIGN)
        ad_sb = keep.tile([P, S // LIST_ROWS], U16, name="ad_sb", align_bytes=ALIGN)
        x_table = keep.tile([P, T], I32, name="x_table", align_bytes=ALIGN)
        xs_table = keep.tile([P, T], U8, name="xs_table", align_bytes=ALIGN)
        w_raw = [keep.tile([P, 2 * N], U8, name="w_raw%d" % w, align_bytes=ALIGN) for w in range(2)]
        ws_raw = keep.tile([P, 2 * N], U8, name="ws_raw", align_bytes=ALIGN)
        w1_raw = keep.tile([P, PACK, H], F32, name="w1_raw", align_bytes=ALIGN)
        gains = [keep.tile([P, U], F32, name="gain%d" % t, align_bytes=ALIGN) for t in range(PACK)]
        xs = keep.tile([P, S], U8, name="xs", align_bytes=ALIGN)
        ws = keep.tile([P, 2 * N], U8, name="ws", align_bytes=ALIGN)

        nc.gpsimd.memset(ws_raw[:].bitcast(I32), 0)
        for tile in (xs_table, xs, ws):
            nc.vector.memset(tile[:].bitcast(I32), 0)

        def move_scales(dst, src):
            for r in range(4):
                nc.sync.dma_start(dst[r:P:32, :].bitcast(I32), src[8 * r : P : 32, :].bitcast(I32))

        gain_rows = gain.rearrange("(p t) u -> p t u", t=PACK)
        nc.sync.dma_start(offs_sb[:], offs)
        nc.scalar.dma_start(w_raw[0][:].bitcast(I32), w2_words[0].bitcast(I32))
        nc.sync.dma_start(ad_sb[:], ad)
        nc.scalar.dma_start(w_raw[1][:].bitcast(I32), w3_words[0].bitcast(I32))
        nc.sync.dma_start(xs_table[0:P:8, :].bitcast(I32), x_scales[0].bitcast(I32))
        nc.scalar.dma_start(ws_raw[0:P:8, span(0, N)].bitcast(I32), w2_scales[0].bitcast(I32))
        nc.scalar.dma_start(ws_raw[0:P:8, span(1, N)].bitcast(I32), w3_scales[0].bitcast(I32))
        nc.sync.dma_start(w1_raw[:], w1.rearrange("(p j) c -> p j c", j=PACK))
        nc.sync.dma_start(x_table[:], x_words[0].rearrange("p n t -> p (n t)").bitcast(I32))

        w_dealt = []

        def deal_words(w, name):
            w_dealt.append(keep.tile([P, PACK, 2 * P], U8, name=name, align_bytes=ALIGN))
            nc.vector.tensor_copy(
                w_dealt[w][:].bitcast(U16),
                w_raw[w][:].bitcast(U16).rearrange("p (m t) -> p t m", t=PACK),
            )

        deal_words(0, "w2_dealt")
        xs_picked = keep.tile([P, S], U8, name="xs_picked", align_bytes=ALIGN)
        nc.vector.tensor_copy(xs_picked[:], xs_table[:].indirect(offs_sb[:]))
        move_scales(xs, xs_picked)

        w1_pairs = w1_raw[:].rearrange("p j (m u e) -> p u m e j", u=2, e=2)
        w1_bf = [keep.tile([P, 2, P, PACK], BF16, name="w1_bf%d" % u, align_bytes=ALIGN) for u in range(2)]
        w1_q = [keep.tile([P, 2 * P], U32, name="w1_q%d" % u, align_bytes=ALIGN) for u in range(2)]
        w1_s = keep.tile([P, PACK * P], U8, name="w1_s", align_bytes=ALIGN)
        nc.vector.tensor_copy(w1_bf[0][:].rearrange("p e m j -> p m e j"), w1_pairs[:, 0])
        nc.scalar.activation(w1_bf[1][:].rearrange("p e m j -> p m e j"), w1_pairs[:, 1], COPY)

        def quantise_w1(u):
            nc.vector.quantize_mx(
                out=w1_q[u][:].bitcast(FP8X4),
                scales=w1_s[:, span(u, 2 * P)],
                in_=w1_bf[u][:].rearrange("p e m j -> p (e m j)"),
            )

        ws_dealt = keep.tile([P, 2 * N], U8, name="ws_dealt", align_bytes=ALIGN)
        nc.vector.tensor_copy(
            ws_dealt[:].rearrange("p (w t m) -> p w t m", w=2, t=PACK),
            ws_raw[:].rearrange("p (w m t) -> p w t m", w=2, t=PACK),
        )
        deal_words(1, "xs_table")
        quantise_w1(0)
        quantise_w1(1)
        for t in range(PACK):
            if t == 3:
                move_scales(ws, ws_dealt)
            nc.sync.dma_start(gains[t][:], gain_rows[:, t, :])

        xq = keep.tile([P, S], I32, name="xq", align_bytes=ALIGN)

        def entries(lists, cols):
            return lists[:, cols.start // LIST_ROWS : cols.stop // LIST_ROWS]

        chunks = [span(c, CHUNK) for c in range(CHUNKS)]
        halves = [span(half, HALF) for half in range(2)]
        inner = slice(CHUNK, CHUNK + HALF)
        outer = (0, CHUNKS - 1)
        for cols in (chunks[0], chunks[3], inner):
            nc.vector.tensor_copy(xq[:, cols].bitcast(U32), x_table[:].bitcast(U32).indirect(entries(offs_sb, cols)))

        psum = ctx.enter_context(tc.psum_pool(name="psum", bufs=1))

        def hidden(t, cols, h_bank):
            nc.tensor.matmul_mx(
                out=h_bank,
                lhsT=w1_q[t // 2][:, span(t % 2, P)].bitcast(FP8X4),
                lhsT_scale=w1_s[:, span(t, P)],
                rhs=xq[:, cols].bitcast(FP8X4),
                rhs_scale=xs[:, cols],
                start=True,
                stop=True,
            )

        h = {}
        pieces = [(t, c) for t in range(PACK) for c in outer]
        for bank, groups in enumerate([[pieces[0:2]], [pieces[2:5]], [pieces[5:8]]]):
            h_bank = psum.tile([P, 3, CHUNK], F32, name="bank%d" % bank)
            for slot, (t, c) in enumerate(sum(groups, [])):
                hidden(t, chunks[c], h_bank[:, slot, :])
            first = 0
            for group in groups:
                h_sb = keep.tile([P, len(group), CHUNK], F32, name="h%d%d" % group[0], align_bytes=ALIGN)
                nc.scalar.activation(h_sb[:], h_bank[:, first : first + len(group), :], RELU)
                for slot, piece in enumerate(group):
                    h[piece] = h_sb[:, slot, :]
                first = first + len(group)
        held = {}
        for c, bank in ((1, 3), (2, 2)):
            held[c] = psum.tile([P, PACK, CHUNK], F32, name="bank%d" % bank)
            for t in range(PACK):
                hidden(t, chunks[c], held[c][:, t, :])

        z_tile = keep.tile([P, CHUNK + PACK * HALF], F32, name="z", align_bytes=ALIGN)
        z = z_tile[:, CHUNK:].rearrange("p (t n) -> p t n", t=PACK)
        picked = keep.tile([P, PACK, HALF], F32, name="picked", align_bytes=ALIGN)

        def inner_window(t):
            return gains[t][:].indirect(entries(ad_sb, inner))

        def gate(t, c):
            part = chunks[outer.index(c)]
            window = gains[t][:].indirect(entries(ad_sb, chunks[c]))
            nc.vector.tensor_tensor(z[:, t, part], window, h[t, c], MULT)

        nc.vector.tensor_copy(picked[:, 0, :], inner_window(0))
        for t in range(PACK - 1):
            for c in outer:
                gate(t, c)
        for t in range(1, PACK):
            nc.scalar.activation(picked[:, t, :], inner_window(t), COPY)

        order = [0, 1, 3, 2]
        taken = {0: [4, 5], 1: [6, 7], 3: [0, 1], 2: [3, 2]}
        banks = {c: [None, None] for c in order}
        z_bf = {0: keep.tile([P, CHUNK, PACK], BF16, name="z_bf0", align_bytes=ALIGN)[:]}
        z_q = [keep.tile([P, CHUNK], U32, name="z_q%d" % c, align_bytes=ALIGN) for c in range(CHUNKS)]
        z_s = [keep.tile([P, CHUNK], U8, name="z_s%d" % c, align_bytes=ALIGN) for c in range(CHUNKS)]
        y_halves = [keep.tile([P, PACK, HALF], F32, name="y%d" % half, align_bytes=ALIGN) for half in range(2)]
        y = [y_halves[c // 2][:, :, chunks[c % 2]] for c in range(CHUNKS)]
        z_bf[3] = y_halves[0][:, PACK - 1, :].bitcast(BF16).rearrange("p (n t) -> p n t", t=PACK)
        y_bf = keep.tile([P, S * PACK], BF16, name="y_bf", align_bytes=ALIGN)
        y_woven = y_bf[:].rearrange("p (n t) -> p n t", t=PACK)
        y_q = keep.tile([P, S], I32, name="y_q", align_bytes=ALIGN)
        y_s = keep.tile([P, S], U8, name="y_s", align_bytes=ALIGN)
        out_rows = out_0.rearrange("(p t) j -> p t j", t=PACK)
        out_words = out_1[0].rearrange("p n t -> p (n t)").bitcast(I32)

        def weave(copy, dst, src):
            copy(dst.rearrange("p (c i) t -> p c t i", i=RUN), src.rearrange("p t (c i) -> p c t i", i=RUN))

        def quantise(codes, scales, woven):
            nc.vector.quantize_mx(out=codes.bitcast(FP8X4), scales=scales, in_=woven.rearrange("p n t -> p (n t)"))

        def output_pass(w, c, t, codes, scales):
            nc.tensor.matmul_mx(
                out=banks[c][t // 2][:, t % 2, :],
                lhsT=w_dealt[w][:, t, :].bitcast(FP4X4),
                lhsT_scale=ws[:, span(w * PACK + t, P)],
                rhs=codes.bitcast(FP8X4),
                rhs_scale=scales,
                start=(w == 0 and t % 2 == 0),
                stop=(w == 1 and t % 2 == 1),
            )

        def open_bank(c, u):
            banks[c][u] = psum.tile([P, 2, CHUNK], F32, name="bank%d" % taken[c][u])
            for t in (2 * u, 2 * u + 1):
                output_pass(0, c, t, xq[:, chunks[c]], xs[:, chunks[c]])

        for c in order[:-1]:
            for u in range(2):
                open_bank(c, u)

        def weave_z(c, copy, start, stop):
            first = outer.index(c) * CHUNK
            weave(copy, z_bf[c][:, start:stop, :], z[:, :, first + start : first + stop])

        def gate_and_weave(c, planes):
            nc.vector.scalar_tensor_tensor(
                out=z_bf[c][:, :, planes],
                in0=held[c][:, planes, :].rearrange("p t n -> p n t"),
                scalar=0.0,
                in1=picked[:, planes, chunks[c - 1]].rearrange("p t n -> p n t"),
                op0=MAX,
                op1=MULT,
            )

        def adapter(c):
            quantise(z_q[c][:], z_s[c][:], z_bf[c])
            for t in range(PACK):
                output_pass(1, c, t, z_q[c][:], z_s[c][:])

        def empty_bank(c, u, copy):
            copy(y[c][:, span(u, 2), :], banks[c][u][:])

        def store_rows(half, u):
            nc.sync.dma_start(out_rows[:, span(u, 2), halves[half]], y_halves[half][:, span(u, 2), :])

        def weave_y(c):
            weave(nc.vector.tensor_copy, y_woven[:, chunks[c], :], y[c])

        def quantise_y(c):
            quantise(y_q[:, chunks[c]], y_s[:, chunks[c]], y_woven[:, chunks[c], :])

        z_bf[1] = keep.tile([P, CHUNK, PACK], BF16, name="h10", align_bytes=ALIGN)[:]
        gate_and_weave(1, span(0, 2))
        gate(3, 0)
        weave_z(0, nc.scalar.copy, 0, CHUNK // 2)
        gate(3, 3)
        weave_z(0, nc.vector.tensor_copy, CHUNK // 2, CHUNK)
        weave_z(3, nc.scalar.copy, 0, CHUNK)
        z_bf[2] = z_tile[:, : 2 * CHUNK].bitcast(BF16).rearrange("p (n t) -> p n t", t=PACK)
        gate_and_weave(1, span(1, 2))
        open_bank(2, 0)
        adapter(0)
        adapter(1)
        gate_and_weave(2, span(0, PACK))
        open_bank(2, 1)
        adapter(3)
        adapter(2)
        empty_bank(0, 0, nc.scalar.copy)
        empty_bank(1, 0, nc.scalar.copy)
        store_rows(0, 0)
        empty_bank(0, 1, nc.scalar.copy)
        empty_bank(1, 1, nc.vector.tensor_copy)
        store_rows(0, 1)
        for u in range(2):
            empty_bank(3, u, nc.scalar.copy)
            empty_bank(2, u, nc.scalar.copy)
            store_rows(1, u)
        for half in range(2):
            weave_y(2 * half)
            weave_y(2 * half + 1)
            quantise_y(2 * half)
            quantise_y(2 * half + 1)
            nc.sync.dma_start(out_words[:, halves[half]], y_q[:, halves[half]])
        for q in range(QUADRANTS):
            nc.sync.dma_start(out_2[0, span(q, 4), :].bitcast(I32), y_s[scale_partitions(q), :].bitcast(I32))
